import numpy as np, ml_dtypes
CORES = [24,25,26,27,28,29,30,31]
N = 8
import mx_ref
BF = ml_dtypes.bfloat16
def gentries(a):
    return np.ascontiguousarray(a.reshape(8, 16, -1).transpose(0, 2, 1)).reshape(8, -1)
def gtable(e):
    e = np.asarray(e); return np.ascontiguousarray(e.reshape(8, -1, 16).transpose(0, 2, 1)).reshape(128, -1).astype(np.int32)
def gcols(t, e):
    v = np.concatenate([t.reshape(8, 16, -1, 4), np.zeros((8, 16, 1, 4), BF)], axis=2)
    return np.ascontiguousarray(np.stack([v[g][:, e[g]] for g in range(8)])).reshape(128, -1)
def tile(rs):
    return np.stack(rs, axis=2).reshape(128, -1).astype(BF)
def pick(q, e):
    c = np.concatenate([q[0].reshape(128, -1, 4), np.zeros((128, 1, 4), np.uint8)], axis=1); s = np.concatenate([q[1], np.ones((16, 1), np.uint8)], axis=1)
    return (np.ascontiguousarray(c[:, e].reshape(128, -1)), np.ascontiguousarray(s[:, e]))
def join(*qs):
    return (np.concatenate([q[0] for q in qs], axis=1), np.concatenate([q[1] for q in qs], axis=1))
def put(q, e, v):
    c, s = q[0].reshape(128, -1, 4).copy(), q[1].copy(); c[:, e] = v[0].reshape(128, -1, 4); s[:, e] = v[1]
    return (c.reshape(128, -1), s)
def pk(c, s):
    return (np.ascontiguousarray(c), mx_ref.live(s))
def emit(q):
    return q[0], q[1]
def packed(v, rng):
    q = [mx_ref.quantize(np.ascontiguousarray(v[r])) for r in range(N)]
    return np.stack([a for a, b in q]), np.stack([mx_ref.plane(b, rng) for a, b in q])
def values_of_codes():
    e, c = np.zeros((128, 128, 4), np.float32), np.zeros((128, 2, 4), np.uint8)
    e[np.arange(128), np.arange(128), 0] = 1
    c[:127, :, 0] = np.arange(256).reshape(2, 128).T[:127]
    return mx_ref.matmul(mx_ref.quantize(e.reshape(128, 512).astype(BF)), (c.reshape(128, 8), np.full((16, 2), 127, np.uint8))).T.reshape(-1).astype(np.float64)
CODE_VALUE, SCALE_VALUE = values_of_codes(), 2.0 ** (np.arange(256) - 127.0)
def decode(q):
    return (CODE_VALUE[q[0]].reshape(16, 8, -1, 4) * SCALE_VALUE[q[1]][:, None, :, None] + 0.0).reshape(128, -1).astype(np.float32)
def f(rng, *shape):
    return mx_ref.flush((rng.standard_normal(shape, dtype=np.float32) * np.exp2(rng.integers(-2, 3, shape[:-1] + (1,)))).astype(BF))
def wide(rng, *shape, cols=0):
    v = rng.standard_normal(shape, dtype=np.float32) * np.exp2(rng.integers(-12, 13, shape)).astype(np.float32)
    if cols: v *= np.repeat(np.exp2(rng.integers(-cols, cols + 1, shape[:-2] + (1, shape[-1] // 4))) * (rng.random(shape[:-2] + (1, shape[-1] // 4)) > 0.0625), 4, axis=-1).astype(np.float32)
    return mx_ref.flush(v.astype(BF))
C, H = 320, 160
STEP = [1, 2, 4]
def numbers_of(rng):
    return {"x": np.array(f(rng, N, 128, 4 * C)), "u": np.array(f(rng, N, 128, 512)), "v": np.array(f(rng, N, 128, 512))}
def lists(rng):
    e = np.tile(np.arange(C), (N, 8, 1))
    q = rng.permuted(e, axis=2)
    p = np.zeros((N, 8, C), np.int64)
    np.put_along_axis(p, q, np.ascontiguousarray(q.reshape(N, 8, H, 2)[..., ::-1]).reshape(N, 8, C), axis=2)
    return rng.permuted(e, axis=2), p
def stored(n, p):
    return {k: np.stack([gtable(e[r]) for r in range(N)]) for k, e in (("nx", n), ("iv", np.argsort(n, axis=2)), ("pr", p))}
def layer(rng, still=[]):
    w = np.array(f(rng, 128, 2048)).reshape(8, 16, 4, 8, 16, 4)
    for i in still:
        w[:, i] = 0
        w[:, :, :, :, i] = 0
    return w
def weights(rng, w):
    c, s = packed(np.stack([np.ascontiguousarray(w).reshape(128, 2048)] * N), rng)
    return {"wc": c, "ws": s}
def setup_inputs(rng):
    return {**numbers_of(rng), **stored(*lists(rng)), **weights(rng, layer(rng))}
def setup_inputs_ties(rng):
    d = numbers_of(rng)
    n, p = lists(rng)
    o = rng.permutation(N)
    k = rng.integers(-1, 2, (N, 8, C))
    k[o[1]] = 1
    k[o[2]] = 1
    t = rng.integers(0, 2, (8, C))
    t = np.where(np.arange(C) < p[o[3]], t, 1 - np.take_along_axis(t, p[o[3]], axis=1))
    k[o[3]] = np.where(t == 1, 1, rng.integers(-1, 1, (8, C)))
    a = np.exp2(rng.integers(-3, 4, (8, 1)).astype(np.float32))
    x = d["x"].reshape(N, 8, 16, C, 4)
    x[:, :, 0] = 0
    x[:, :, 0, :, 0] = k.astype(np.float32).astype(BF)
    x[:, :, 8:] = 0
    x[:, :, 8, :, 0] = (-1.125 * a).astype(BF)
    x[:, :, 10, :, 0] = (-0.0703125 * a).astype(BF)
    u = d["u"].reshape(N, 128, 128, 4)
    u[:, :, ::16] = 0
    for r in range(N):
        for h in range(0, 128, 16): u[r, h, h, 0] = 0.0 if r == o[0] else -1.0 if r == o[2] else 1.0
    w = layer(rng, [0])
    w[:, :, :, :, 8:] = 0
    for g in range(8):
        w[g, 8, 0, g, 8, 0] = -28.0
        for b in range(4): w[g, 10, b, g, 9, 0] = -2.0 ** (b - 5)
    return {"x": x.reshape(N, 128, 4 * C), "u": u.reshape(N, 128, 512), "v": d["v"], **stored(n, p), **weights(rng, w)}
def setup_inputs_near(rng):
    d = numbers_of(rng)
    k = np.where(rng.permutation(N) % 2 == 0, 2.0 ** -30, 1.0)
    x = rng.choice([-1.0, 1.0], (N, 8, 16, C, 4)) * (1.0 + 0.125 * rng.integers(0, 8, (N, 8, 16, C, 4))) * 64.0 * k[:, None, None, None, None]
    x[:, :, :9] = 0
    s = rng.integers(-1, 2, (N, 8, C)) * k[:, None, None]
    x[:, :, 0, :, 0] = 1.125 * s
    x[:, :, 1, :, 0] = -1.25 * s
    x[:, :, 7, :, 0] = k[:, None, None]
    x[:, :, 8, :, 0] = rng.choice([-1.0, 1.0], (N, 8, C)) * k[:, None, None]
    x[:, :, 9, :, 0] = 64.0 * k[:, None, None]
    for r in range(N):
        at = [0, C - 1, int(rng.integers(C)), int(rng.integers(C))]
        for g, j in zip(rng.permutation(8)[:4], at): x[r, g, 0, j, 0] = 2.0 ** 30 * rng.choice([-1.0, 1.0])
    u = d["u"].reshape(N, 128, 128, 4)
    u[:, :, ::16] = 0
    for h in range(0, 128, 16):
        u[:, h, h, 0] = (1.125 * k).astype(np.float32).astype(BF)
        u[:, h + 1, h, 0] = k.astype(np.float32).astype(BF)
        u[:, h + 2, h, 0] = k.astype(np.float32).astype(BF)
    w = layer(rng, list(range(10)))
    for g in range(8):
        w[g, 8, 0, g, 2, 0] = 2.0 ** -8
        w[g, 9, 0, g, 7, 0] = 1.0
    return {"x": x.astype(np.float32).reshape(N, 128, 4 * C).astype(BF), "u": u.reshape(N, 128, 512), "v": d["v"], **stored(*lists(rng)), **weights(rng, w)}
def setup_inputs_odd(rng):
    d = numbers_of(rng)
    x = (1.0 + (2 * rng.integers(0, 64, (N, 16, 8, C, 4)) + 1) * 2.0 ** -7) * np.exp2(-rng.integers(0, 7, (N, 16, 8, C, 4)).astype(np.float64)) * rng.choice([-1.0, 1.0], (N, 16, 8, C, 4))
    x[:, :, 0, :, 0] = rng.choice([1.96875, 1.875], (N, 16, C)) * 2.0 ** 8 * rng.choice([-1.0, 1.0], (N, 16, C))
    k = np.exp2(rng.integers(0, 4, (N, 8, C)) - 5.0)
    r = int(rng.integers(N))
    k[r] = k[r, :1].copy()
    x[:, ::2, 1, :, 0] = k * (1.0 + 0.125 * rng.integers(0, 2, (N, 8, C)))
    x[:, ::2, 2, :, 0] = k
    x[r, 0, 1, :, 0] = k[r, 0]
    u = d["u"].reshape(N, 16, 8, 128, 4)
    u[:, :, :, ::16] = 0
    for g in range(8):
        u[:, 2 * g, 1, 16 * g, 0] = 1.0
        u[:, 2 * g, 2, 16 * g, 0] = -1.0
    for g, i, e in ((0, 1, 4), (3, 2, 2)):
        u[r, :, :, 16 * g] = 0
        u[r, 0, i, 16 * g, 0] = 1.0
        u[r, 2 * e, 1, 16 * g, 0] = 1.875 * 2.0 ** -25
        u[r, 14, 2, 16 * g, 0] = -1.0
    return {"x": x.astype(np.float32).reshape(N, 128, 4 * C).astype(BF), "u": u.reshape(N, 128, 512), "v": d["v"], **stored(*lists(rng)), **weights(rng, layer(rng, [0, 1, 2, 8]))}
def setup_inputs_ends(rng):
    d = numbers_of(rng)
    o, e = rng.permutation(N) % 4, rng.permutation(N) % 4
    c = rng.choice([-1.0, 1.0], (N, C))
    c[:, H:] = -c[:, :H][:, ::-1]
    s = rng.choice([-1.0, 1.0], (N, 128, C, 4))
    s[o == 0] = -1
    s[o == 1] = c[o == 1][:, None, :, None]
    s[o == 3] = s[o == 3][:, :, :1]
    x = s * (0.63 + 0.06 * rng.random((N, 128, C, 4))) * 2.0 ** 30
    x[o == 3] = s[o == 3] * 2.0 ** -26
    x[o == 3, 48:64] = s[o == 3, 48:64] * 2.0 ** -30
    x[:, 120:] = s[:, 120:] * 2.0 ** -29
    a = np.stack([rng.permutation(8) % 2 * 2.0 - 1.0 for r in range(N)]) * np.where(o < 2, 2.0 ** 30, 2.0 ** -30)[:, None]
    u = d["u"].reshape(N, 128, 128, 4)
    u[:, :, ::16] = a.astype(np.float32).astype(BF)[:, None, :, None]
    v = rng.choice([-1.0, 1.0], (N, 128, 512)) * np.where(o % 2 == 0, 2.0 ** 30, 2.0 ** -30)[:, None, None]
    n, p = lists(rng)
    i = np.arange(C)
    p[o == 0] = i ^ 1
    p[o == 1] = C - 1 - i
    p[o == 2] = (i + H) % C
    n[e == 0] = i
    n[e == 1] = C - 1 - i
    n[e == 2] = (i + 1) % C
    n[e == 3] = p[e == 3]
    w = np.zeros((128, 4, 128, 4), np.float32)
    j = np.arange(128)
    for b in range(4): w[j, b, j, b] = np.where(j // 16 == 3, 0.0, np.where(j < 120, -4.0, 256.0))
    return {"x": x.astype(np.float32).reshape(N, 128, 4 * C).astype(BF), "u": u.reshape(N, 128, 512), "v": v.astype(np.float32).astype(BF), **stored(n, p), **weights(rng, w.astype(BF))}
def setup_inputs_spread(rng):
    d = setup_inputs(rng)
    d["x"] = wide(rng, N, 128, 4 * C, cols=6)
    return d
def check_inputs(d):
    b = []
    for k in ("x", "u", "v"):
        a = np.abs(d[k].astype(np.float32))
        if not (np.isfinite(a).all() and ((a == 0) | (a >= 2.0 ** -30) & (a <= 2.0 ** 30)).all()): b.append("a value of " + k)
    none, least, most = [emit(mx_ref.quantize(np.full((128, 16), k, np.float32).astype(BF)))[1][0, 0] for k in (0.0, 2.0 ** -8, 2.0 ** 8)]
    full = np.arange(C)
    for k in ("nx", "iv", "pr"):
        if not ((d[k] >= 0) & (d[k] < C)).all(): b.append("an entry of " + k)
    for r in range(N):
        n, i, p = [np.clip(gentries(d[k][r]), 0, C - 1) for k in ("nx", "iv", "pr")]
        if not (np.take_along_axis(i, n, axis=1) == full).all(): b.append("iv: not the inverse of nx")
        if not (np.take_along_axis(p, p, axis=1) == full).all() or (p == full).any(): b.append("pr: not pairs")
        if ((d["wc"][r] == 0x7F) | (d["wc"][r] == 0xFF)).any(): b.append("wc: a code that is no number")
        s = mx_ref.live(d["ws"][r])
        if ((s != none) & ((s < least) | (s > most))).any(): b.append("ws: a scale out of range")
        if (((d["wc"][r].reshape(16, 8, 512, 4) & 0x7F) != 0) & (s == none)[:, None, :, None]).any(): b.append("wc: a code other than zero under the scale of zeros")
        if (d["wc"][r] != d["wc"][0]).any() or (s != mx_ref.live(d["ws"][0])).any(): b.append("wc and ws: not the same on all ranks")
    return b
def reference(x, u, v, nx, iv, pr, wc, ws):
    qu = [mx_ref.quantize(u[r]) for r in range(N)]
    lay = [[pick(pk(wc[r], ws[r]), np.arange(128 * b, 128 * b + 128)) for b in range(4)] for r in range(N)]
    nxt, inv, pair = [[gentries(t[r]).astype(np.int64) for r in range(N)] for t in (nx, iv, pr)]
    now = [x[r] for r in range(N)]
    for step in STEP:
        had, made = [], []
        for r in range(N):
            n, m = nxt[r], inv[r]
            q = mx_ref.quantize(now[r])
            had.append(decode(q).astype(BF))
            bit = mx_ref.matmul(qu[r], q)[::16] > 0
            t = np.where(bit == np.take_along_axis(bit, pair[r], axis=1), pair[r], np.arange(C))
            for g in (0, 2, 4, 6, 1, 3, 5, 7):
                h = (g + 1) % 8
                w = n[g][t[g][m[g]]]
                n[g], m[g] = n[g][t[g]], t[g][m[g]]
                n[h], m[h] = n[h][w], w[m[h]]
            one = gcols(had[r], n).astype(np.float32)
            two = gcols(had[r], np.take_along_axis(n, n, axis=1)).astype(np.float32)
            z = mx_ref.quantize(((one + two) * np.float32(0.5)).astype(BF))
            made.append(mx_ref.quantize(tile([mx_ref.matmul(lay[r][b], z) * np.float32(0.03125) for b in range(4)])))
        for r in range(N):
            k = decode(join(pick(made[r], np.arange(H)), pick(made[r ^ step], np.arange(H, C)))).astype(BF)
            now[r] = (had[r].astype(np.float32) + gcols(k, inv[r]).astype(np.float32)).astype(BF)
    y, nl = np.zeros((N, 128, C), np.float32), np.zeros((N, 8, C), np.float32)
    oc, osc = np.zeros((N, 128, 4 * C), np.uint8), np.zeros((N, 16, C), np.uint8)
    for r in range(N):
        q = mx_ref.quantize(now[r])
        y[r] = mx_ref.matmul(mx_ref.quantize(v[r]), q)
        nl[r] = nxt[r]
        oc[r], osc[r] = emit(q)
    return {"y": y, "nl": nl, "oc": oc, "osc": osc}

@@ -1,0 +1,288 @@
+from concourse.mybir import dt, AluOpType, ActivationFunctionType
+import comms_topo
+
+C, HF = 320, 160
+ROUNDS = 3
+STEP = [1, 2, 4]
+BF, F32, I32, U16, U8, MXC = "bfloat16", "float32", "int32", "uint16", "uint8", "float8_e4m3fn_x4"
+
+
+def _scratch():
+    s = {}
+
+    def sb(dtype, **kw):
+        for k, n in kw.items():
+            s[k] = ("sbuf", [128, n], dtype)
+    sb(BF, xin=1280, xst=1280, zt=1280, ho=640, hp=640, ut=512, vt=512, et=528, fw=1280, gw=1280, g2=1280, xw=1280)
+    sb(BF, idr=C, mk=C, mko=C, rr=C, d0=C, thr=C)
+    sb(BF, ner=C, ngr=C, p1=C, sge=C, sgg=C, sge2=C, sgg2=C, eqe=C, eqg=C, sce=C, scg=C, nep=C, wer=C, b1=C, b2=C)
+    sb(BF, alm=C, als=C, ngm=C, ngs=C, wpm=C, wps=C, nem=C, nes=C, tgr=C, wr=C, wt=C, mgm=C, mgs=C, mem=C, mes=C)
+    sb(F32, yo=C, nlf=C, nle=C, al=20, de=20, dg=20, ef=60, gf=60, t1=60, t2=60, mev=2, mod=2, pmf=2)
+    sb(F32, ea=20, eb=20, ec=20, ga=20, gb=20, gc=20, fa=20, fb=20, ha=20, hb=20, hc=20)
+    sb(I32, own=60, shd=60, upd=60, jp=C, j16=C, pc=2, pa=2, pb=2, ai=20, ui=16)
+    sb(U16, lle=60, llg=60, ne=20, me=20, mg=20, te=20, tg=20, aL=20, ws_=20, nL=20, mL=20, ul=16)
+    sb(MXC, tq=C, zq=C, hqo=HF, hqp=HF, uq=128, uu=256, vq=128, wq=512, eq0=128, eq1=128, eq2=128, eq3=128)
+    sb(U8, ts=C, zs=C, hso=HF, hsp=HF, us=128, uus=256, vs=128, wsp=512, es0=128, es1=128, es2=128, es3=128)
+    for k in range(ROUNDS):
+        s["lq%d" % k] = ("sbuf", [128, HF], MXC)
+        s["ls%d" % k] = ("sbuf", [128, HF], U8)
+    s["ps"] = ("psum", [128, 512 * 8], F32)
+    return s
+
+
+SCRATCH = _scratch()
+SEMAPHORES = ["qv", "qs", "qp", "qg"] + ["arr%d" % k for k in range(ROUNDS)] + ["loc%d" % k for k in range(ROUNDS)] + ["dm%d" % k for k in range(48)]
+
+
+def rank_program(g, core, T, topo):
+    rank = T.rank_of(core)
+    if rank is None:
+        return
+    A = AluOpType
+    CP, SG = ActivationFunctionType.Copy, ActivationFunctionType.Sign
+    V, S, P = g.vector, g.scalar, g.tensor
+    queue = {"v": V, "s": S, "p": P, "g": g, "y": g.sync}
+    semof = {"v": "qv", "s": "qs", "p": "qp", "g": "qg"}
+    cnt = {}
+    known = {q: {} for q in queue}
+    writer, readers, ndma = {}, {}, [0]
+
+    def need(q, tok):
+        if known[q].get(tok[1], 0) < tok[2]:
+            queue[q].wait_ge(T.sem[tok[1]], tok[2])
+            known[q][tok[1]] = tok[2]
+        for k, n in tok[3].items():
+            if known[q].get(k, 0) < n: known[q][k] = n
+
+    def order(q, who, reads, writes):
+        toks = []
+        for k in reads:
+            if k in writer: toks.append(writer[k])
+            if k[:2] == "ps": toks += [t for t in readers.get(k, []) if t[0] != who]
+        for k in writes:
+            if k in writer and writer[k][0] != who: toks.append(writer[k])
+            toks += [t for t in readers.get(k, []) if t[0] != who]
+        for t in sorted(toks, key=lambda t: -t[2]): need(q, t)
+
+    def note(tok, reads, writes):
+        for k in reads: readers.setdefault(k, []).append(tok)
+        for k in writes:
+            writer[k] = tok
+            readers[k] = []
+
+    def emit(q, fn, reads, writes):
+        order(q, q, reads, writes)
+        s = semof[q]
+        cnt[s] = cnt.get(s, 0) + 1
+        fn(queue[q]).then_inc(T.sem[s], 1)
+        note((q, s, cnt[s], dict(known[q])), reads, writes)
+
+    def dma(q, out, in_, reads, writes):
+        s = "dm%d" % ndma[0]
+        ndma[0] += 1
+        order(q, s, reads, writes)
+        queue[q].dma_start(out, in_).then_inc(T.sem[s], 16)
+        note((s, s, 16, dict(known[q])), reads, writes)
+
+    def vv(fn, r, w): emit("v", fn, r, w)
+    def tt(out, in0, in1, op, r, w): vv(lambda e: e.tensor_tensor(out, in0, in1, op), r, w)
+    def tsc(out, in0, s1, s2, ops, r, w): vv(lambda e: e.tensor_scalar(out, in0, s1, s2, *ops), r, w)
+    def cp(out, in_, r, w): vv(lambda e: e.tensor_copy(out, in_), r, w)
+    def act(out, in_, r, w, scale=1.0): emit("s", lambda e: e.activation(out, in_, CP, scale=scale), r, w)
+    def quant(c, s, t, r, w): vv(lambda e: e.quantize_mx(c, s, t), r, w)
+
+    def mm(bank, n, a, sa, b, sb, r):
+        emit("p", lambda e: e.matmul_mx(T.ps[:, 512 * bank:512 * bank + n], a, sa, b, sb, True, True), r, ["ps%d" % bank])
+
+    def bank(i, n): return T.ps[:, 512 * i:512 * i + n]
+    def off(name, lo=0, hi=20): return T[name][:, lo:hi]
+    def row(name): return T[name][:]
+
+    def comp(out, win, lst, lo=0):
+        act(row(out), row(win).indirect(off(lst, lo, lo + 20)), [win, lst], [out])
+
+    def compv(out, win, lst, lo=0):
+        cp(row(out), row(win).indirect(off(lst, lo, lo + 20)), [win, lst], [out])
+
+    def compm(out, sc, win, lst, mask="mk", lo=0):
+        tt(row(out), row(win).indirect(off(lst, lo, lo + 20)), row(mask), A.mult, [win, lst, mask], [out])
+        vv(lambda e: e.tensor_tensor_scan(row(sc), row("rr"), row(out), 0.0, A.mult, A.add), ["rr", out], [sc])
+
+    def ends(sc): return T[sc][:, 15:C:16]
+    def tolist(lst, sc): tsc(T[lst][:], ends(sc), 160.0, None, [A.add], [sc], [lst])
+
+    vv(lambda e: e.memset(T.shd[:], 0), [], ["shd"])
+    vv(lambda e: e.memset(T.upd[:], 0), [], ["upd"])
+    vv(lambda e: e.memset(T.et[:], 0.5), [], ["et"])
+    dma("y", T.xin[:, 0:640], T.x[:, 0:640], [], ["xin0"])
+    dma("s", T.xin[:, 640:1280], T.x[:, 640:1280], [], ["xin1"])
+    dma("y", T.ut[:], T.u[:], [], ["ut"])
+    for i, src in enumerate((T.nx, T.iv, T.pr)):
+        c = slice(20 * i, 20 * i + 20)
+        dma("s", T.own[:, c], src[:], [], ["own%d" % i])
+        dma("s" if i == 0 else "y", T.shd[16:128, c], src[0:112, :], ["shd"], ["shd%d" % i])
+        dma("y", T.upd[0:112, c], src[16:128, :], ["upd"], ["upd%d" % i])
+    dma("y", T.wq[:].bitcast(dt.uint8), T.wc[:], [], ["wq"])
+    dma("y", T.wsp[:], T.ws[:], [], ["wsp"])
+    dma("y", T.vt[:], T.v[:], [], ["vt"])
+
+    def gg(fn, r, w): emit("g", fn, r, w)
+    gg(lambda e: e.iota(T.pc[:, 0:1], [[0, 1]], 0, 1), [], ["pc"])
+    gg(lambda e: e.iota(T.ui[:], [[16, 2], [32, 4], [0, 2]], 0, 0), [], ["ui"])
+    gg(lambda e: e.iota(T.ai[:], [[16, 20]], 0, 0), [], ["ai"])
+    gg(lambda e: e.iota(T.jp[:], [[1, C]], 128, -1), [], ["jp"])
+    gg(lambda e: e.iota(T.j16[:], [[0, 20], [1, 16]], 0, 0), [], ["j16"])
+    gg(lambda e: e.affine_select(T.et[:], T.et[:], [[-1, 528]], A.is_equal, 0.0, 3, 4), ["et"], ["et"])
+    gg(lambda e: e.iota(T.idr[:], [[1, C]], -160, 0, allow_small_or_imprecise_dtypes=True), [], ["idr"])
+    tsc(T.pa[:, 0:1], T.pc[:, 0:1], 15, None, [A.bitwise_and], ["pc"], ["pa"])
+    tsc(T.pb[:, 0:1], T.pc[:, 0:1], 31, None, [A.bitwise_and], ["pc"], ["pb"])
+    cp(T.pmf[:, 0:1], T.pa[:, 0:1], ["pa"], ["pmf"])
+    tsc(T.mev[:, 0:1], T.pb[:, 0:1], 16, None, [A.is_lt], ["pb"], ["mev"])
+    tsc(T.mod[:, 0:1], T.pb[:, 0:1], 16, None, [A.is_ge], ["pb"], ["mod"])
+    cp(T.ul[:], T.ui[:], ["ui"], ["ul"])
+    tsc(T.al[:], T.ai[:], T.pmf[:, 0:1], None, [A.add], ["ai", "pmf"], ["al"])
+    tsc(T.jp[:], T.jp[:], 15, None, [A.bitwise_and], ["jp"], ["jp"])
+    tsc(row("mk"), T.jp[:], 0, None, [A.is_equal], ["jp"], ["mk"])
+    tsc(row("d0"), T.jp[:], 0, 2.0, [A.not_equal, A.mult], ["jp"], ["d0"])
+    tsc(row("rr"), T.j16[:], 0, None, [A.not_equal], ["j16"], ["rr"])
+    tsc(row("mko"), row("mk"), T.mod[:, 0:1], None, [A.mult], ["mk", "mod"], ["mko"])
+    vv(lambda e: e.tensor_tensor_scan(row("thr"), row("d0"), row("mk"), 0.0, A.mult, A.max), ["d0", "mk"], ["thr"])
+    ow, sh, up = ["own0", "own1", "own2"], ["shd0", "shd1", "shd2"], ["upd0", "upd1", "upd2"]
+    tt(T.t1[:], T.own[:], T.shd[:], A.subtract, ow + sh, ["t1"])
+    tt(T.t2[:], T.upd[:], T.own[:], A.subtract, ow + up, ["t2"])
+    tsc(T.t1[:], T.t1[:], T.mev[:, 0:1], None, [A.mult], ["t1", "mev"], ["t1"])
+    tsc(T.t2[:], T.t2[:], T.mev[:, 0:1], None, [A.mult], ["t2", "mev"], ["t2"])
+    tt(T.ef[:], T.t1[:], T.shd[:], A.add, ["t1"] + sh, ["ef"])
+    tt(T.gf[:], T.t2[:], T.own[:], A.add, ["t2"] + ow, ["gf"])
+    cp(T.lle[:], T.ef[:], ["ef"], ["lle"])
+    cp(T.llg[:], T.gf[:], ["gf"], ["llg"])
+    cp(T.me[:], T.ef[:, 20:40], ["ef"], ["me"])
+    cp(T.mg[:], T.gf[:, 20:40], ["gf"], ["mg"])
+    tt(T.de[:], T.ef[:, 40:60], T.al[:], A.subtract, ["ef", "al"], ["de"])
+    tt(T.dg[:], T.gf[:, 40:60], T.al[:], A.subtract, ["gf", "al"], ["dg"])
+    comp("ner", "idr", "lle")
+    comp("ngr", "idr", "llg")
+    comp("p1", "ngr", "lle")
+    quant(T.uq[:], T.us[:], T.ut[:], ["ut"], ["uq"])
+    cp(T.uu[:].bitcast(dt.uint32), T.uq[:].bitcast(dt.uint32).indirect(T.ul[:]), ["uq", "ul"], ["uu"])
+    cp(T.uus[:], T.us[:].indirect(T.ul[:]), ["uq", "ul"], ["uus"])
+    for b in range(4):
+        quant(T["eq%d" % b][:], T["es%d" % b][:], T.et[:, 3 - b:515 - b], ["et"], ["eq%d" % b])
+    quant(T.tq[:], T.ts[:], T.xin[:], ["xin0", "xin1"], ["tq"])
+
+    def turns(eq, sc, s, lst, p, d, x):
+        cp(row(s + "2"), row(s), [s], [s + "2"])
+        tt(row(eq), row(s).indirect(off(p, 40, 60)), row(s + "2"), A.is_equal, [s, s + "2", p], [eq])
+        vv(lambda e: e.tensor_tensor_scan(row(sc), row("d0"), row(eq), 0.0, A.mult, A.max), ["d0", eq], [sc])
+        tsc(T[x + "a"][:], ends(sc), T.thr[:, 15:16], None, [A.is_ge], [sc, "thr"], [x + "a"])
+        tt(T[x + "b"][:], T[x + "a"][:], T[d][:], A.mult, [x + "a", d], [x + "b"])
+        tt(T[x + "c"][:], T[x + "b"][:], T.al[:], A.add, [x + "b", "al"], [x + "c"])
+        cp(T[lst][:], T[x + "c"][:], [x + "c"], [lst])
+
+    def win(name, b): return T[name][:, C * b:C * b + C]
+
+    def layer(tile, hq, hs, src, plane, c0, keys, banks, on_s):
+        for b in range(4):
+            mm(banks + b, HF, T.wq[:, 128 * b:128 * b + 128], T.wsp[:, 128 * b:128 * b + 128], T[src][:, c0:c0 + HF], T[plane][:, c0:c0 + HF], ["wq", "wsp"] + keys)
+        for b in range(4):
+            o, i, r, w = T[tile][:, b:640:4], bank(banks + b, HF), ["ps%d" % (banks + b)], ["%s.%d" % (tile, b)]
+            if b in on_s: act(o, i, r, w, 0.03125)
+            else: tsc(o, i, 0.03125, None, [A.mult], r, w)
+        quant(T[hq][:], T[hs][:], T[tile][:], ["%s.%d" % (tile, b) for b in range(4)], [hq])
+
+    def unpack(hq, hs, h):
+        for b in range(4):
+            mm(b, HF, T["eq%d" % b][:], T["es%d" % b][:], T[hq][:], T[hs][:], ["eq%d" % b, hq])
+        for b in range(4):
+            c = slice(C * b + HF * h, C * b + HF * h + HF)
+            tt(T.xw[:, c], T.gw[:, c], bank(b, HF), A.add, ["gw%d" % b, "ps%d" % b], ["xw%d.%d" % (b, h)])
+
+    for k in range(ROUNDS):
+        last = k == ROUNDS - 1
+        partner = T.cores[rank ^ STEP[k]]
+        mm(4, C, T.uu[:, 0:128], T.uus[:, 0:128], T.tq[:], T.ts[:], ["uu", "uus", "tq"])
+        mm(5, C, T.uu[:, 128:256], T.uus[:, 128:256], T.tq[:], T.ts[:], ["uu", "uus", "tq"])
+        for b in range(4):
+            mm(b, C, T["eq%d" % b][:], T["es%d" % b][:], T.tq[:], T.ts[:], ["eq%d" % b, "tq"])
+        emit("s", lambda e: e.activation(row("sge"), bank(4, C), SG, bias=-(2.0 ** -93)), ["ps4"], ["sge"])
+        emit("s", lambda e: e.activation(row("sgg"), bank(5, C), SG, bias=-(2.0 ** -93)), ["ps5"], ["sgg"])
+        for b in (0, 1): act(win("fw", b), bank(b, C), ["ps%d" % b], ["fw%d" % b])
+        turns("eqe", "sce", "sge", "te", "lle", "de", "e")
+        turns("eqg", "scg", "sgg", "tg", "llg", "dg", "g")
+        comp("nep", "ner", "te")
+        comp("wer", "nep", "me")
+        compv("b1", "p1", "te")
+        compv("b2", "b1", "me")
+        comp("ngr", "b2", "tg")
+        compm("alm", "als", "wer", "mg")
+        tolist("aL", "als")
+        for b in (2, 3): act(win("fw", b), bank(b, C), ["ps%d" % b], ["fw%d" % b])
+        compm("wpm", "wps", "ngr", "aL")
+        for a in range(4):
+            c = 32 * ((a + 1) % 4)
+            tsc(T.ws_[c:c + 32, :], T.wps[32 * a:32 * a + 32, 15:C:16], 160.0, None, [A.add], ["wps"], ["ws_%d" % a])
+        WS = ["ws_%d" % a for a in range(4)]
+        tt(row("nem"), row("nep").indirect(off("ws_")), row("mk"), A.mult, ["nep", "mk"] + WS, ["nem"])
+        vv(lambda e: e.tensor_tensor_scan(row("nes"), row("rr"), row("nem"), 0.0, A.mult, A.add), ["rr", "nem"], ["nes"])
+        compm("ngm", "ngs", "b2", "tg", "mko")
+        tsc(T.fa[:], ends("nes"), T.mev[:, 0:1], 160.0, [A.mult, A.add], ["nes", "mev"], ["fa"])
+        tt(T.fb[:], T.fa[:], ends("ngs"), A.add, ["fa", "ngs"], ["fb"])
+        cp(T.nL[:], T.fb[:], ["fb"], ["nL"])
+        for b in (0, 2, 3): act(win("gw", b), win("fw", b).indirect(off("nL")), ["fw%d" % b, "nL"], ["gw%d" % b])
+        cp(win("gw", 1), win("fw", 1).indirect(off("nL")), ["fw1", "nL"], ["gw1"])
+        for h in (1, 0):
+            for b in range(4):
+                c0 = C * b + HF * h
+                cp(T.g2[:, c0:c0 + HF], T.gw[:, c0:c0 + HF], ["gw%d" % b], ["g2%d.%d" % (b, h)])
+                tt(T.zt[:, 640 * h + b:640 * h + 640:4], win("gw", b).indirect(off("nL", 10 * h, 10 * h + 10)), T.g2[:, c0:c0 + HF], A.add, ["gw%d" % b, "g2%d.%d" % (b, h), "nL"], ["zt%d.%d" % (h, b)])
+            c = slice(HF * h, HF * h + HF)
+            quant(T.zq[:, c], T.zs[:, c], T.zt[:, 640 * h:640 * h + 640], ["zt%d.%d" % (h, b) for b in range(4)], ["zq%d" % h])
+            if h == 1:
+                rid, pid, _ = topo.addr(partner)
+                eng = topo.engines(core, partner)
+                lo, hi = sum(1 << i for i in eng[:8]), sum(1 << i for i in eng[-8:])
+                order("g", "remote", ["zq1"], [])
+                lq, ls, arr, loc = T["lq%d" % k], T["ls%d" % k], T.sem["arr%d" % k], T.sem["loc%d" % k]
+                g.remote_dma(lq[:].bitcast(dt.uint8), T.zq[:, c].bitcast(dt.uint8), arr, loc, pid, rid, lo)
+                g.remote_dma(ls[:], T.zs[:, c], arr, loc, pid, rid, hi)
+                note(("remote", "loc%d" % k, 16, {}), ["zq1"], [])
+                note(("remote", "arr%d" % k, 16, {}), [], ["lq%d" % k])
+        comp("tgr", "idr", "tg")
+        act(row("wr"), row("idr").indirect(off("ws_")), ["idr"] + WS, ["wr"])
+        comp("wt", "wr", "te")
+        compm("mgm", "mgs", "tgr", "aL")
+        compm("mem", "mes", "wt", "me")
+        if not last:
+            tolist("mg", "mgs")
+            tolist("me", "mes")
+            tolist("ne", "nes")
+        tsc(T.ha[:], ends("mes"), T.mev[:, 0:1], 160.0, [A.mult, A.add], ["mes", "mev"], ["ha"])
+        tsc(T.hb[:], ends("mgs"), T.mod[:, 0:1], None, [A.mult], ["mgs", "mod"], ["hb"])
+        tt(T.hc[:], T.ha[:], T.hb[:], A.add, ["ha", "hb"], ["hc"])
+        cp(T.mL[:], T.hc[:], ["hc"], ["mL"])
+        layer("ho", "hqo", "hso", "zq", "zs", 0, ["zq0"], 4, (0, 1, 2, 3))
+        unpack("hqo", "hso", 0)
+        act(row("ner"), row("nep").indirect(off("ws_")), ["nep"] + WS, ["ner"])
+        if not last: comp("p1", "ngr", "ne")
+        if last:
+            tsc(T.nle[:], row("ner"), 160.0, None, [A.add], ["ner"], ["nle"])
+            tsc(T.nlf[:], row("ngr"), 160.0, None, [A.add], ["ngr"], ["nlf"])
+            dma("y", T.nl[0:8:2, :], T.nle[0:128:32, :], ["nle"], [])
+            dma("y", T.nl[1:8:2, :], T.nlf[0:128:32, :], ["nlf"], [])
+            quant(T.vq[:], T.vs[:], T.vt[:], ["vt"], ["vq"])
+        layer("hp", "hqp", "hsp", "lq%d" % k, "ls%d" % k, 0, ["lq%d" % k], 4, (0, 1))
+        unpack("hqp", "hsp", 1)
+        for b in (0, 1): act(T.xst[:, b:1280:4], win("xw", b).indirect(off("mL")), ["xw%d.0" % b, "xw%d.1" % b, "mL"], ["xst%d" % b], 2.0)
+        for b in (2, 3): tsc(T.xst[:, b:1280:4], win("xw", b).indirect(off("mL")), 2.0, None, [A.mult], ["xw%d.0" % b, "xw%d.1" % b, "mL"], ["xst%d" % b])
+        quant(T.tq[:], T.ts[:], T.xst[:], ["xst%d" % b for b in range(4)], ["tq"])
+
+    dma("y", T.oc[:], T.tq[:].bitcast(dt.uint8), ["tq"], [])
+    for i in range(4): dma("s", T.osc[4 * i:4 * i + 4, :], T.ts[32 * i:32 * i + 4, :], ["tq"], [])
+    mm(6, C, T.vq[:], T.vs[:], T.tq[:], T.ts[:], ["vq", "tq"])
+    cp(T.yo[:], bank(6, C), ["ps6"], ["yo"])
+    dma("y", T.y[:], T.yo[:], ["yo"], [])
+    for i in range(ndma[0]): need("g", ("x", "dm%d" % i, 16, {}))
+    for s, n in cnt.items(): need("g", ("x", s, n, {}))
+    for k in range(ROUNDS):
+        need("g", ("x", "loc%d" % k, 16, {}))
+        need("g", ("x", "arr%d" % k, 16, {}))

@@ -13,14 +13,14 @@ def _scratch():
     def sb(dtype, **kw):
         for k, n in kw.items():
             s[k] = ("sbuf", [128, n], dtype)
-    sb(BF, xin=1280, xst=1280, zt=1280, ho=640, hp=640, ut=512, vt=512, et=528, fw=1280, gw=1280, g2=1280, xw=1280)
-    sb(BF, idr=C, mk=C, mko=C, rr=C, d0=C, thr=C)
-    sb(BF, ner=C, ngr=C, p1=C, sge=C, sgg=C, sge2=C, sgg2=C, eqe=C, eqg=C, sce=C, scg=C, nep=C, wer=C, b1=C, b2=C)
-    sb(BF, alm=C, als=C, ngm=C, ngs=C, wpm=C, wps=C, nem=C, nes=C, tgr=C, wr=C, wt=C, mgm=C, mgs=C, mem=C, mes=C)
-    sb(F32, yo=C, nlf=C, nle=C, al=20, de=20, dg=20, ef=60, gf=60, t1=60, t2=60, mev=2, mod=2, pmf=2)
-    sb(F32, ea=20, eb=20, ec=20, ga=20, gb=20, gc=20, fa=20, fb=20, ha=20, hb=20, hc=20)
-    sb(I32, own=60, shd=60, upd=60, jp=C, j16=C, pc=2, pa=2, pb=2, ai=20, ui=16)
-    sb(U16, lle=60, llg=60, ne=20, me=20, mg=20, te=20, tg=20, aL=20, ws_=20, nL=20, mL=20, ul=16)
+    sb(BF, xin=1280, xst=1280, zt=1280, ho=640, hp=640, ut=512, vt=512, et=516, fw=1280, gw=1280, g2=1280, xw=1280)
+    sb(BF, idr=C, mk=C, rr=C, d0=C, thr=C, j16=C)
+    sb(BF, ner=C, ngr=C, p1=C, sge=C, sgg=C, spe=C, spg=C, s1=640, s2=640, nep=C, wer=C, b1=C, b2=C)
+    sb(BF, alm=C, ngm=C, as_=640, rw=C, nem=C, nes=C, tgr=C, wr=C, wr2=C, wt=C, mgm=C, mgs=C, mem=C, mes=C)
+    sb(F32, yo=C, nlf=C, nle=C, al=20, dd=40, dd2=40, pp=40, ef=60, gf=60, t1=60, t2=60, mev=2, mod=2, pmf=2)
+    sb(F32, q1=40, qc=40, qd=40, ba=40, cc=40, q2=40, qm=40, qt=40, fa=20, fb=20, fz=20, ha=20, hb=20, hc=20)
+    sb(I32, own=60, shd=60, upd=60, jp=C, pc=2, pa=2, pb=2, ai=20, ui=16)
+    sb(U16, lle=60, llg=60, ne=20, me=20, mg=20, te=20, tg=20, aL=20, sh=40, nL=20, mL=20, ul=16)
     sb(MXC, tq=C, zq=C, hqo=HF, hqp=HF, uq=128, uu=256, vq=128, wq=512, eq0=128, eq1=128, eq2=128, eq3=128)
     sb(U8, ts=C, zs=C, hso=HF, hsp=HF, us=128, uus=256, vs=128, wsp=512, es0=128, es1=128, es2=128, es3=128)
     for k in range(ROUNDS):
@@ -85,68 +85,69 @@ def rank_program(g, core, T, topo):
         note((s, s, 16, dict(known[q])), reads, writes)
 
     def vv(fn, r, w): emit("v", fn, r, w)
+    def gg(fn, r, w): emit("g", fn, r, w)
     def tt(out, in0, in1, op, r, w): vv(lambda e: e.tensor_tensor(out, in0, in1, op), r, w)
     def tsc(out, in0, s1, s2, ops, r, w): vv(lambda e: e.tensor_scalar(out, in0, s1, s2, *ops), r, w)
     def cp(out, in_, r, w): vv(lambda e: e.tensor_copy(out, in_), r, w)
-    def act(out, in_, r, w, scale=1.0): emit("s", lambda e: e.activation(out, in_, CP, scale=scale), r, w)
+    def act(out, in_, r, w, scale=1.0): emit("s", lambda e: e.activation(out, in_, CP) if scale == 1.0 else e.activation(out, in_, CP, scale=scale), r, w)
     def quant(c, s, t, r, w): vv(lambda e: e.quantize_mx(c, s, t), r, w)
+    def scan(out, d, x, op, r, w): vv(lambda e: e.tensor_tensor_scan(out, d, x, 0.0, A.mult, op), r, w)
 
     def mm(bank, n, a, sa, b, sb, r):
         emit("p", lambda e: e.matmul_mx(T.ps[:, 512 * bank:512 * bank + n], a, sa, b, sb, True, True), r, ["ps%d" % bank])
 
     def bank(i, n): return T.ps[:, 512 * i:512 * i + n]
-    def off(name, lo=0, hi=20): return T[name][:, lo:hi]
+    def win(name, b): return T[name][:, C * b:C * b + C]
     def row(name): return T[name][:]
+    def ends(name, lo=0, hi=C): return T[name][:, lo + 15:hi:16]
 
-    def comp(out, win, lst, lo=0):
-        act(row(out), row(win).indirect(off(lst, lo, lo + 20)), [win, lst], [out])
+    def comp(out, w, lst, lo=0, key=None):
+        act(row(out), row(w).indirect(T[lst][:, lo:lo + 20]), [w] + (key or [lst]), [out])
 
-    def compv(out, win, lst, lo=0):
-        cp(row(out), row(win).indirect(off(lst, lo, lo + 20)), [win, lst], [out])
+    def compv(out, w, lst, lo=0):
+        cp(row(out), row(w).indirect(T[lst][:, lo:lo + 20]), [w, lst], [out])
 
-    def compm(out, sc, win, lst, mask="mk", lo=0):
-        tt(row(out), row(win).indirect(off(lst, lo, lo + 20)), row(mask), A.mult, [win, lst, mask], [out])
-        vv(lambda e: e.tensor_tensor_scan(row(sc), row("rr"), row(out), 0.0, A.mult, A.add), ["rr", out], [sc])
+    def compm(out, w, lst, lo=0, key=None):
+        tt(row(out), row(w).indirect(T[lst][:, lo:lo + 20]), row("mk"), A.mult, [w, "mk"] + (key or [lst]), [out])
 
-    def ends(sc): return T[sc][:, 15:C:16]
-    def tolist(lst, sc): tsc(T[lst][:], ends(sc), 160.0, None, [A.add], [sc], [lst])
+    def sums(sc, x, lo=0): scan(T[sc][:, lo:lo + C], row("rr"), row(x), A.add, ["rr", x], [sc + "%d" % lo])
+    def tolist(l, sc): tsc(T[l][:], ends(sc), 160.0, None, [A.add], [sc + "0"], [l])
 
     vv(lambda e: e.memset(T.shd[:], 0), [], ["shd"])
     vv(lambda e: e.memset(T.upd[:], 0), [], ["upd"])
     vv(lambda e: e.memset(T.et[:], 0.5), [], ["et"])
-    dma("y", T.xin[:, 0:640], T.x[:, 0:640], [], ["xin0"])
-    dma("s", T.xin[:, 640:1280], T.x[:, 640:1280], [], ["xin1"])
     dma("y", T.ut[:], T.u[:], [], ["ut"])
-    for i, src in enumerate((T.nx, T.iv, T.pr)):
-        c = slice(20 * i, 20 * i + 20)
-        dma("s", T.own[:, c], src[:], [], ["own%d" % i])
-        dma("s" if i == 0 else "y", T.shd[16:128, c], src[0:112, :], ["shd"], ["shd%d" % i])
-        dma("y", T.upd[0:112, c], src[16:128, :], ["upd"], ["upd%d" % i])
+    dma("y", T.xin[:, 0:640], T.x[:, 0:640], [], ["xin0"])
+    lists = (T.pr, T.nx, T.iv)
+    for i, src in enumerate(lists): dma("s", T.own[:, 20 * i:20 * i + 20], src[:], [], ["own%d" % i])
+    for i, src in enumerate(lists): dma("s", T.shd[16:128, 20 * i:20 * i + 20], src[0:112, :], ["shd"], ["shd%d" % i])
+    for i, src in enumerate(lists): dma("s", T.upd[0:112, 20 * i:20 * i + 20], src[16:128, :], ["upd"], ["upd%d" % i])
+    dma("y", T.xin[:, 640:1280], T.x[:, 640:1280], [], ["xin1"])
     dma("y", T.wq[:].bitcast(dt.uint8), T.wc[:], [], ["wq"])
     dma("y", T.wsp[:], T.ws[:], [], ["wsp"])
     dma("y", T.vt[:], T.v[:], [], ["vt"])
 
-    def gg(fn, r, w): emit("g", fn, r, w)
     gg(lambda e: e.iota(T.pc[:, 0:1], [[0, 1]], 0, 1), [], ["pc"])
     gg(lambda e: e.iota(T.ui[:], [[16, 2], [32, 4], [0, 2]], 0, 0), [], ["ui"])
     gg(lambda e: e.iota(T.ai[:], [[16, 20]], 0, 0), [], ["ai"])
     gg(lambda e: e.iota(T.jp[:], [[1, C]], 128, -1), [], ["jp"])
-    gg(lambda e: e.iota(T.j16[:], [[0, 20], [1, 16]], 0, 0), [], ["j16"])
-    gg(lambda e: e.affine_select(T.et[:], T.et[:], [[-1, 528]], A.is_equal, 0.0, 3, 4), ["et"], ["et"])
+    gg(lambda e: e.affine_select(T.et[:], T.et[:], [[-1, 516]], A.is_equal, 0.0, 3, 4), ["et"], ["et"])
     gg(lambda e: e.iota(T.idr[:], [[1, C]], -160, 0, allow_small_or_imprecise_dtypes=True), [], ["idr"])
+    gg(lambda e: e.iota(T.j16[:], [[0, 20], [1, 16]], 0, 0, allow_small_or_imprecise_dtypes=True), [], ["j16"])
     tsc(T.pa[:, 0:1], T.pc[:, 0:1], 15, None, [A.bitwise_and], ["pc"], ["pa"])
     tsc(T.pb[:, 0:1], T.pc[:, 0:1], 31, None, [A.bitwise_and], ["pc"], ["pb"])
+    cp(T.ul[:], T.ui[:], ["ui"], ["ul"])
     cp(T.pmf[:, 0:1], T.pa[:, 0:1], ["pa"], ["pmf"])
     tsc(T.mev[:, 0:1], T.pb[:, 0:1], 16, None, [A.is_lt], ["pb"], ["mev"])
     tsc(T.mod[:, 0:1], T.pb[:, 0:1], 16, None, [A.is_ge], ["pb"], ["mod"])
-    cp(T.ul[:], T.ui[:], ["ui"], ["ul"])
     tsc(T.al[:], T.ai[:], T.pmf[:, 0:1], None, [A.add], ["ai", "pmf"], ["al"])
     tsc(T.jp[:], T.jp[:], 15, None, [A.bitwise_and], ["jp"], ["jp"])
     tsc(row("mk"), T.jp[:], 0, None, [A.is_equal], ["jp"], ["mk"])
-    tsc(row("d0"), T.jp[:], 0, 2.0, [A.not_equal, A.mult], ["jp"], ["d0"])
-    tsc(row("rr"), T.j16[:], 0, None, [A.not_equal], ["j16"], ["rr"])
-    tsc(row("mko"), row("mk"), T.mod[:, 0:1], None, [A.mult], ["mk", "mod"], ["mko"])
-    vv(lambda e: e.tensor_tensor_scan(row("thr"), row("d0"), row("mk"), 0.0, A.mult, A.max), ["d0", "mk"], ["thr"])
+    tsc(row("d0"), row("mk"), -2.0, 2.0, [A.mult, A.add], ["mk"], ["d0"])
+    quant(T.uq[:], T.us[:], T.ut[:], ["ut"], ["uq"])
+    cp(T.uu[:].bitcast(dt.uint32), T.uq[:].bitcast(dt.uint32).indirect(T.ul[:]), ["uq", "ul"], ["uu"])
+    act(T.uus[:], T.us[:].indirect(T.ul[:]), ["uq", "ul"], ["uus"])
+    quant(T.tq[:], T.ts[:], T.xin[:], ["xin0", "xin1"], ["tq"])
     ow, sh, up = ["own0", "own1", "own2"], ["shd0", "shd1", "shd2"], ["upd0", "upd1", "upd2"]
     tt(T.t1[:], T.own[:], T.shd[:], A.subtract, ow + sh, ["t1"])
     tt(T.t2[:], T.upd[:], T.own[:], A.subtract, ow + up, ["t2"])
@@ -156,36 +157,24 @@ def rank_program(g, core, T, topo):
     tt(T.gf[:], T.t2[:], T.own[:], A.add, ["t2"] + ow, ["gf"])
     cp(T.lle[:], T.ef[:], ["ef"], ["lle"])
     cp(T.llg[:], T.gf[:], ["gf"], ["llg"])
-    cp(T.me[:], T.ef[:, 20:40], ["ef"], ["me"])
-    cp(T.mg[:], T.gf[:, 20:40], ["gf"], ["mg"])
-    tt(T.de[:], T.ef[:, 40:60], T.al[:], A.subtract, ["ef", "al"], ["de"])
-    tt(T.dg[:], T.gf[:, 40:60], T.al[:], A.subtract, ["gf", "al"], ["dg"])
-    comp("ner", "idr", "lle")
-    comp("ngr", "idr", "llg")
-    comp("p1", "ngr", "lle")
-    quant(T.uq[:], T.us[:], T.ut[:], ["ut"], ["uq"])
-    cp(T.uu[:].bitcast(dt.uint32), T.uq[:].bitcast(dt.uint32).indirect(T.ul[:]), ["uq", "ul"], ["uu"])
-    cp(T.uus[:], T.us[:].indirect(T.ul[:]), ["uq", "ul"], ["uus"])
+    scan(row("thr"), row("d0"), row("mk"), A.max, ["d0", "mk"], ["thr"])
+    for i, (f, l) in enumerate((("ef", "lle"), ("gf", "llg"))):
+        c = slice(20 * i, 20 * i + 20)
+        cp(T.pp[:, c], T[f][:, 0:20], [f], ["pp%d" % i])
+        tt(T.dd[:, c], T[f][:, 0:20], T.al[:], A.subtract, [f, "al"], ["dd%d" % i])
+    tsc(T.dd2[:], T.dd[:], 2.0, None, [A.mult], ["dd0", "dd1"], ["dd2"])
     for b in range(4):
         quant(T["eq%d" % b][:], T["es%d" % b][:], T.et[:, 3 - b:515 - b], ["et"], ["eq%d" % b])
-    quant(T.tq[:], T.ts[:], T.xin[:], ["xin0", "xin1"], ["tq"])
+    tsc(row("rr"), row("j16"), 0, None, [A.not_equal], ["j16"], ["rr"])
+    comp("ner", "idr", "lle", 20)
+    comp("ngr", "idr", "llg", 20)
+    comp("p1", "ngr", "lle", 20)
 
-    def turns(eq, sc, s, lst, p, d, x):
-        cp(row(s + "2"), row(s), [s], [s + "2"])
-        tt(row(eq), row(s).indirect(off(p, 40, 60)), row(s + "2"), A.is_equal, [s, s + "2", p], [eq])
-        vv(lambda e: e.tensor_tensor_scan(row(sc), row("d0"), row(eq), 0.0, A.mult, A.max), ["d0", eq], [sc])
-        tsc(T[x + "a"][:], ends(sc), T.thr[:, 15:16], None, [A.is_ge], [sc, "thr"], [x + "a"])
-        tt(T[x + "b"][:], T[x + "a"][:], T[d][:], A.mult, [x + "a", d], [x + "b"])
-        tt(T[x + "c"][:], T[x + "b"][:], T.al[:], A.add, [x + "b", "al"], [x + "c"])
-        cp(T[lst][:], T[x + "c"][:], [x + "c"], [lst])
-
-    def win(name, b): return T[name][:, C * b:C * b + C]
-
-    def layer(tile, hq, hs, src, plane, c0, keys, banks, on_s):
+    def layer(tile, hq, hs, src, plane, keys, on_s):
         for b in range(4):
-            mm(banks + b, HF, T.wq[:, 128 * b:128 * b + 128], T.wsp[:, 128 * b:128 * b + 128], T[src][:, c0:c0 + HF], T[plane][:, c0:c0 + HF], ["wq", "wsp"] + keys)
+            mm(4 + b, HF, T.wq[:, 128 * b:128 * b + 128], T.wsp[:, 128 * b:128 * b + 128], T[src][:, 0:HF], T[plane][:, 0:HF], ["wq", "wsp"] + keys)
         for b in range(4):
-            o, i, r, w = T[tile][:, b:640:4], bank(banks + b, HF), ["ps%d" % (banks + b)], ["%s.%d" % (tile, b)]
+            o, i, r, w = T[tile][:, b:640:4], bank(4 + b, HF), ["ps%d" % (4 + b)], ["%s.%d" % (tile, b)]
             if b in on_s: act(o, i, r, w, 0.03125)
             else: tsc(o, i, 0.03125, None, [A.mult], r, w)
         quant(T[hq][:], T[hs][:], T[tile][:], ["%s.%d" % (tile, b) for b in range(4)], [hq])
@@ -200,41 +189,77 @@ def rank_program(g, core, T, topo):
     for k in range(ROUNDS):
         last = k == ROUNDS - 1
         partner = T.cores[rank ^ STEP[k]]
-        mm(4, C, T.uu[:, 0:128], T.uus[:, 0:128], T.tq[:], T.ts[:], ["uu", "uus", "tq"])
-        mm(5, C, T.uu[:, 128:256], T.uus[:, 128:256], T.tq[:], T.ts[:], ["uu", "uus", "tq"])
+        mel, mgl, mlo = ("me", "mg", 0) if k else ("lle", "llg", 40)
+        ue, uf = (T.uu[:, 0:128], T.uus[:, 0:128]), (T.uu[:, 128:256], T.uus[:, 128:256])
+        for h in (0, 1): mm(4 + h, HF, *ue, T.tq[:, HF * h:HF * h + HF], T.ts[:, HF * h:HF * h + HF], ["uu", "uus", "tq"])
+        mm(6, C, *uf, T.tq[:], T.ts[:], ["uu", "uus", "tq"])
         for b in range(4):
             mm(b, C, T["eq%d" % b][:], T["es%d" % b][:], T.tq[:], T.ts[:], ["eq%d" % b, "tq"])
-        emit("s", lambda e: e.activation(row("sge"), bank(4, C), SG, bias=-(2.0 ** -93)), ["ps4"], ["sge"])
-        emit("s", lambda e: e.activation(row("sgg"), bank(5, C), SG, bias=-(2.0 ** -93)), ["ps5"], ["sgg"])
-        for b in (0, 1): act(win("fw", b), bank(b, C), ["ps%d" % b], ["fw%d" % b])
-        turns("eqe", "sce", "sge", "te", "lle", "de", "e")
-        turns("eqg", "scg", "sgg", "tg", "llg", "dg", "g")
+        emit("s", lambda e: e.activation(T.sge[:, 0:HF], bank(4, HF), SG, bias=-(2.0 ** -93)), ["ps4"], ["sge0"])
+        tsc(T.sge[:, HF:C], bank(5, HF), 0.0, None, [A.is_gt], ["ps5"], ["sge1"])
+        tsc(row("sgg"), bank(6, C), 0.0, None, [A.is_gt], ["ps6"], ["sgg"])
+        act(row("spe"), row("sge").indirect(T.lle[:, 0:20]), ["sge0", "sge1", "lle"], ["spe"])
+        comp("spg", "sgg", "llg")
+        act(win("fw", 0), bank(0, C), ["ps0"], ["fw0"])
+        scan(T.s1[:, 0:C], row("d0"), row("sge"), A.max, ["d0", "sge0", "sge1"], ["s10"])
+        scan(T.s1[:, C:640], row("d0"), row("sgg"), A.max, ["d0", "sgg"], ["s11"])
+        tsc(T.q1[:], ends("s1", 0, 640), T.thr[:, 15:16], None, [A.is_ge], ["s10", "s11", "thr"], ["q1"])
+        tt(T.qc[:], T.q1[:], T.dd[:], A.mult, ["q1", "dd0", "dd1"], ["qc"])
+        tt(T.qd[:], T.q1[:], T.dd2[:], A.mult, ["q1", "dd2"], ["qd"])
+        tt(T.ba[:], T.pp[:], T.qc[:], A.subtract, ["pp0", "pp1", "qc"], ["ba"])
+        tt(T.cc[:], T.qd[:], T.dd[:], A.subtract, ["qd", "dd0", "dd1"], ["cc"])
+
+        def turns(i, sp, lst):
+            c, x = slice(20 * i, 20 * i + 20), "%d" % i
+            scan(T.s2[:, C * i:C * i + C], row("d0"), row(sp), A.max, ["d0", sp], ["s2" + x])
+            yield
+            tsc(T.q2[:, c], ends("s2", C * i, C * i + C), T.thr[:, 15:16], None, [A.is_ge], ["s2" + x, "thr"], ["q2" + x])
+            yield
+            tt(T.qm[:, c], T.q2[:, c], T.cc[:, c], A.mult, ["q2" + x, "cc"], ["qm" + x])
+            yield
+            tt(T.qt[:, c], T.qm[:, c], T.ba[:, c], A.add, ["qm" + x, "ba"], ["qt" + x])
+            yield
+            cp(T[lst][:], T.qt[:, c], ["qt" + x], [lst])
+            yield
+        e, f = turns(0, "spe", "te"), turns(1, "spg", "tg")
+        for w in "eeeefef": next(e if w == "e" else f)
         comp("nep", "ner", "te")
-        comp("wer", "nep", "me")
+        comp("wer", "nep", mel, mlo)
+        for b in (1, 2, 3): act(win("fw", b), bank(b, C), ["ps%d" % b], ["fw%d" % b])
         compv("b1", "p1", "te")
-        compv("b2", "b1", "me")
-        comp("ngr", "b2", "tg")
-        compm("alm", "als", "wer", "mg")
-        tolist("aL", "als")
-        for b in (2, 3): act(win("fw", b), bank(b, C), ["ps%d" % b], ["fw%d" % b])
-        compm("wpm", "wps", "ngr", "aL")
+        next(f)
+        compv("b2", "b1", mel, mlo)
+        next(f)
+        next(f)
+        compm("alm", "wer", mgl, mlo)
+        compm("ngm", "b2", "tg")
+        sums("as_", "alm", 0)
+        sums("as_", "ngm", C)
         for a in range(4):
             c = 32 * ((a + 1) % 4)
-            tsc(T.ws_[c:c + 32, :], T.wps[32 * a:32 * a + 32, 15:C:16], 160.0, None, [A.add], ["wps"], ["ws_%d" % a])
-        WS = ["ws_%d" % a for a in range(4)]
-        tt(row("nem"), row("nep").indirect(off("ws_")), row("mk"), A.mult, ["nep", "mk"] + WS, ["nem"])
-        vv(lambda e: e.tensor_tensor_scan(row("nes"), row("rr"), row("nem"), 0.0, A.mult, A.add), ["rr", "nem"], ["nes"])
-        compm("ngm", "ngs", "b2", "tg", "mko")
-        tsc(T.fa[:], ends("nes"), T.mev[:, 0:1], 160.0, [A.mult, A.add], ["nes", "mev"], ["fa"])
-        tt(T.fb[:], T.fa[:], ends("ngs"), A.add, ["fa", "ngs"], ["fb"])
+            tsc(T.sh[c:c + 32, :], T.as_[32 * a:32 * a + 32, 15:640:16], 160.0, None, [A.add], ["as_0", "as_%d" % C], ["sh%d" % a])
+        SH = ["sh%d" % a for a in range(4)]
+        comp("tgr", "idr", "tg")
+        comp("rw", "nep", "sh", 20, SH)
+        comp("ner", "rw", "sh", 0, SH)
+        comp("wr", "idr", "sh", 20, SH)
+        tsc(T.aL[:], ends("as_"), 160.0, None, [A.add], ["as_0"], ["aL"])
+        tsc(T.fz[:], ends("as_", C, 640), T.mod[:, 0:1], None, [A.mult], ["as_%d" % C, "mod"], ["fz"])
+        compm("mgm", "tgr", "aL")
+        compm("nem", "rw", "sh", 0, SH)
+        sums("mgs", "mgm")
+        sums("nes", "nem")
+        tsc(T.fa[:], ends("nes"), T.mev[:, 0:1], 160.0, [A.mult, A.add], ["nes0", "mev"], ["fa"])
+        tt(T.fb[:], T.fa[:], T.fz[:], A.add, ["fa", "fz"], ["fb"])
         cp(T.nL[:], T.fb[:], ["fb"], ["nL"])
-        for b in (0, 2, 3): act(win("gw", b), win("fw", b).indirect(off("nL")), ["fw%d" % b, "nL"], ["gw%d" % b])
-        cp(win("gw", 1), win("fw", 1).indirect(off("nL")), ["fw1", "nL"], ["gw1"])
+        for b in (0, 2, 3): act(win("gw", b), win("fw", b).indirect(T.nL[:]), ["fw%d" % b, "nL"], ["gw%d" % b])
+        cp(win("gw", 1), win("fw", 1).indirect(T.nL[:]), ["fw1", "nL"], ["gw1"])
         for h in (1, 0):
-            for b in range(4):
-                c0 = C * b + HF * h
-                cp(T.g2[:, c0:c0 + HF], T.gw[:, c0:c0 + HF], ["gw%d" % b], ["g2%d.%d" % (b, h)])
-                tt(T.zt[:, 640 * h + b:640 * h + 640:4], win("gw", b).indirect(off("nL", 10 * h, 10 * h + 10)), T.g2[:, c0:c0 + HF], A.add, ["gw%d" % b, "g2%d.%d" % (b, h), "nL"], ["zt%d.%d" % (h, b)])
+            for b in (1, 0, 2, 3):
+                c = slice(C * b + HF * h, C * b + HF * h + HF)
+                if h: cp(T.g2[:, c], T.gw[:, c], ["gw%d" % b], ["g2%d.%d" % (b, h)])
+                else: act(T.g2[:, c], T.gw[:, c], ["gw%d" % b], ["g2%d.%d" % (b, h)])
+                tt(T.zt[:, 640 * h + b:640 * h + 640:4], win("gw", b).indirect(T.nL[:, 10 * h:10 * h + 10]), T.g2[:, c], A.add, ["gw%d" % b, "g2%d.%d" % (b, h), "nL"], ["zt%d.%d" % (h, b)])
             c = slice(HF * h, HF * h + HF)
             quant(T.zq[:, c], T.zs[:, c], T.zt[:, 640 * h:640 * h + 640], ["zt%d.%d" % (h, b) for b in range(4)], ["zq%d" % h])
             if h == 1:
@@ -247,40 +272,38 @@ def rank_program(g, core, T, topo):
                 g.remote_dma(ls[:], T.zs[:, c], arr, loc, pid, rid, hi)
                 note(("remote", "loc%d" % k, 16, {}), ["zq1"], [])
                 note(("remote", "arr%d" % k, 16, {}), [], ["lq%d" % k])
-        comp("tgr", "idr", "tg")
-        act(row("wr"), row("idr").indirect(off("ws_")), ["idr"] + WS, ["wr"])
-        comp("wt", "wr", "te")
-        compm("mgm", "mgs", "tgr", "aL")
-        compm("mem", "mes", "wt", "me")
+        comp("wr2", "wr", "sh", 0, SH)
+        comp("wt", "wr2", "te")
+        comp("ngr", "b2", "tg")
         if not last:
-            tolist("mg", "mgs")
-            tolist("me", "mes")
             tolist("ne", "nes")
-        tsc(T.ha[:], ends("mes"), T.mev[:, 0:1], 160.0, [A.mult, A.add], ["mes", "mev"], ["ha"])
-        tsc(T.hb[:], ends("mgs"), T.mod[:, 0:1], None, [A.mult], ["mgs", "mod"], ["hb"])
+            tolist("mg", "mgs")
+        tsc(T.hb[:], ends("mgs"), T.mod[:, 0:1], None, [A.mult], ["mgs0", "mod"], ["hb"])
+        compm("mem", "wt", mel, mlo)
+        layer("ho", "hqo", "hso", "zq", "zs", ["zq0"], (0, 1, 2, 3))
+        if not last: comp("p1", "ngr", "ne")
+        sums("mes", "mem")
+        tsc(T.ha[:], ends("mes"), T.mev[:, 0:1], 160.0, [A.mult, A.add], ["mes0", "mev"], ["ha"])
+        if not last: tolist("me", "mes")
         tt(T.hc[:], T.ha[:], T.hb[:], A.add, ["ha", "hb"], ["hc"])
         cp(T.mL[:], T.hc[:], ["hc"], ["mL"])
-        layer("ho", "hqo", "hso", "zq", "zs", 0, ["zq0"], 4, (0, 1, 2, 3))
         unpack("hqo", "hso", 0)
-        act(row("ner"), row("nep").indirect(off("ws_")), ["nep"] + WS, ["ner"])
-        if not last: comp("p1", "ngr", "ne")
-        if last:
-            tsc(T.nle[:], row("ner"), 160.0, None, [A.add], ["ner"], ["nle"])
-            tsc(T.nlf[:], row("ngr"), 160.0, None, [A.add], ["ngr"], ["nlf"])
-            dma("y", T.nl[0:8:2, :], T.nle[0:128:32, :], ["nle"], [])
-            dma("y", T.nl[1:8:2, :], T.nlf[0:128:32, :], ["nlf"], [])
-            quant(T.vq[:], T.vs[:], T.vt[:], ["vt"], ["vq"])
-        layer("hp", "hqp", "hsp", "lq%d" % k, "ls%d" % k, 0, ["lq%d" % k], 4, (0, 1))
+        layer("hp", "hqp", "hsp", "lq%d" % k, "ls%d" % k, ["lq%d" % k], (0, 2))
         unpack("hqp", "hsp", 1)
-        for b in (0, 1): act(T.xst[:, b:1280:4], win("xw", b).indirect(off("mL")), ["xw%d.0" % b, "xw%d.1" % b, "mL"], ["xst%d" % b], 2.0)
-        for b in (2, 3): tsc(T.xst[:, b:1280:4], win("xw", b).indirect(off("mL")), 2.0, None, [A.mult], ["xw%d.0" % b, "xw%d.1" % b, "mL"], ["xst%d" % b])
+        for b in (0, 1): act(T.xst[:, b:1280:4], win("xw", b).indirect(T.mL[:]), ["xw%d.0" % b, "xw%d.1" % b, "mL"], ["xst%d" % b], 2.0)
+        for b in (2, 3): tsc(T.xst[:, b:1280:4], win("xw", b).indirect(T.mL[:]), 2.0, None, [A.mult], ["xw%d.0" % b, "xw%d.1" % b, "mL"], ["xst%d" % b])
         quant(T.tq[:], T.ts[:], T.xst[:], ["xst%d" % b for b in range(4)], ["tq"])
+        if k == 0: quant(T.vq[:], T.vs[:], T.vt[:], ["vt"], ["vq"])
 
     dma("y", T.oc[:], T.tq[:].bitcast(dt.uint8), ["tq"], [])
     for i in range(4): dma("s", T.osc[4 * i:4 * i + 4, :], T.ts[32 * i:32 * i + 4, :], ["tq"], [])
     mm(6, C, T.vq[:], T.vs[:], T.tq[:], T.ts[:], ["vq", "tq"])
+    tsc(T.nle[:], row("ner"), 160.0, None, [A.add], ["ner"], ["nle"])
     cp(T.yo[:], bank(6, C), ["ps6"], ["yo"])
+    dma("y", T.nl[0:8:2, :], T.nle[0:128:32, :], ["nle"], [])
     dma("y", T.y[:], T.yo[:], ["yo"], [])
+    tsc(T.nlf[:], row("ngr"), 160.0, None, [A.add], ["ngr"], ["nlf"])
+    dma("y", T.nl[1:8:2, :], T.nlf[0:128:32, :], ["nlf"], [])
     for i in range(ndma[0]): need("g", ("x", "dm%d" % i, 16, {}))
     for s, n in cnt.items(): need("g", ("x", s, n, {}))
     for k in range(ROUNDS):

@@ -17,8 +17,8 @@ def _scratch():
     sb(BF, idr=C, mk=C, rr=C, d0=C, thr=C, j16=C)
     sb(BF, ner=C, ngr=C, p1=C, sge=C, sgg=C, spe=C, spg=C, s1=640, s2=640, nep=C, wer=C, b1=C, b2=C)
     sb(BF, alm=C, ngm=C, as_=640, rw=C, nem=C, nes=C, tgr=C, wr=C, wr2=C, wt=C, mgm=C, mgs=C, mem=C, mes=C)
-    sb(F32, yo=C, nlf=C, nle=C, al=20, dd=40, dd2=40, pp=40, ef=60, gf=60, t1=60, t2=60, mev=2, mod=2, pmf=2)
-    sb(F32, q1=40, qc=40, qd=40, ba=40, cc=40, q2=40, qm=40, qt=40, fa=20, fb=20, fz=20, ha=20, hb=20, hc=20)
+    sb(F32, yo=C, nlf=C, nle=C, al=20, dd=40, ef=60, gf=60, t1=60, t2=60, mev=2, mod=2, pmf=2)
+    sb(F32, q1=40, qe=40, q2=40, qm=40, qt=40, fa=20, fb=20, fz=20, ha=20, hb=20, hc=20)
     sb(I32, own=60, shd=60, upd=60, jp=C, pc=2, pa=2, pb=2, ai=20, ui=16)
     sb(U16, lle=60, llg=60, ne=20, me=20, mg=20, te=20, tg=20, aL=20, sh=40, nL=20, mL=20, ul=16)
     sb(MXC, tq=C, zq=C, hqo=HF, hqp=HF, uq=128, uu=256, vq=128, wq=512, eq0=128, eq1=128, eq2=128, eq3=128)
@@ -131,8 +131,8 @@ def rank_program(g, core, T, topo):
     gg(lambda e: e.iota(T.ui[:], [[16, 2], [32, 4], [0, 2]], 0, 0), [], ["ui"])
     gg(lambda e: e.iota(T.ai[:], [[16, 20]], 0, 0), [], ["ai"])
     gg(lambda e: e.iota(T.jp[:], [[1, C]], 128, -1), [], ["jp"])
-    gg(lambda e: e.affine_select(T.et[:], T.et[:], [[-1, 516]], A.is_equal, 0.0, 3, 4), ["et"], ["et"])
     gg(lambda e: e.iota(T.idr[:], [[1, C]], -160, 0, allow_small_or_imprecise_dtypes=True), [], ["idr"])
+    gg(lambda e: e.affine_select(T.et[:], T.et[:], [[-1, 516]], A.is_equal, 0.0, 3, 4), ["et"], ["et"])
     gg(lambda e: e.iota(T.j16[:], [[0, 20], [1, 16]], 0, 0, allow_small_or_imprecise_dtypes=True), [], ["j16"])
     tsc(T.pa[:, 0:1], T.pc[:, 0:1], 15, None, [A.bitwise_and], ["pc"], ["pa"])
     tsc(T.pb[:, 0:1], T.pc[:, 0:1], 31, None, [A.bitwise_and], ["pc"], ["pb"])
@@ -144,10 +144,6 @@ def rank_program(g, core, T, topo):
     tsc(T.jp[:], T.jp[:], 15, None, [A.bitwise_and], ["jp"], ["jp"])
     tsc(row("mk"), T.jp[:], 0, None, [A.is_equal], ["jp"], ["mk"])
     tsc(row("d0"), row("mk"), -2.0, 2.0, [A.mult, A.add], ["mk"], ["d0"])
-    quant(T.uq[:], T.us[:], T.ut[:], ["ut"], ["uq"])
-    cp(T.uu[:].bitcast(dt.uint32), T.uq[:].bitcast(dt.uint32).indirect(T.ul[:]), ["uq", "ul"], ["uu"])
-    act(T.uus[:], T.us[:].indirect(T.ul[:]), ["uq", "ul"], ["uus"])
-    quant(T.tq[:], T.ts[:], T.xin[:], ["xin0", "xin1"], ["tq"])
     ow, sh, up = ["own0", "own1", "own2"], ["shd0", "shd1", "shd2"], ["upd0", "upd1", "upd2"]
     tt(T.t1[:], T.own[:], T.shd[:], A.subtract, ow + sh, ["t1"])
     tt(T.t2[:], T.upd[:], T.own[:], A.subtract, ow + up, ["t2"])
@@ -157,26 +153,29 @@ def rank_program(g, core, T, topo):
     tt(T.gf[:], T.t2[:], T.own[:], A.add, ["t2"] + ow, ["gf"])
     cp(T.lle[:], T.ef[:], ["ef"], ["lle"])
     cp(T.llg[:], T.gf[:], ["gf"], ["llg"])
+    comp("ner", "idr", "lle", 20)
+    quant(T.uq[:], T.us[:], T.ut[:], ["ut"], ["uq"])
+    cp(T.uu[:].bitcast(dt.uint32), T.uq[:].bitcast(dt.uint32).indirect(T.ul[:]), ["uq", "ul"], ["uu"])
+    act(T.uus[:], T.us[:].indirect(T.ul[:]), ["uq", "ul"], ["uus"])
+    for h in (0, 1): quant(T.tq[:, HF * h:HF * h + HF], T.ts[:, HF * h:HF * h + HF], T.xin[:, 640 * h:640 * h + 640], ["xin%d" % h], ["tq%d" % h])
     scan(row("thr"), row("d0"), row("mk"), A.max, ["d0", "mk"], ["thr"])
     for i, (f, l) in enumerate((("ef", "lle"), ("gf", "llg"))):
         c = slice(20 * i, 20 * i + 20)
-        cp(T.pp[:, c], T[f][:, 0:20], [f], ["pp%d" % i])
         tt(T.dd[:, c], T[f][:, 0:20], T.al[:], A.subtract, [f, "al"], ["dd%d" % i])
-    tsc(T.dd2[:], T.dd[:], 2.0, None, [A.mult], ["dd0", "dd1"], ["dd2"])
-    for b in range(4):
-        quant(T["eq%d" % b][:], T["es%d" % b][:], T.et[:, 3 - b:515 - b], ["et"], ["eq%d" % b])
-    tsc(row("rr"), row("j16"), 0, None, [A.not_equal], ["j16"], ["rr"])
-    comp("ner", "idr", "lle", 20)
     comp("ngr", "idr", "llg", 20)
-    comp("p1", "ngr", "lle", 20)
 
-    def layer(tile, hq, hs, src, plane, keys, on_s):
+    def unpackers():
+        for b in range(4):
+            quant(T["eq%d" % b][:], T["es%d" % b][:], T.et[:, 3 - b:515 - b], ["et"], ["eq%d" % b])
+
+    def layer(tile, hq, hs, src, plane, keys, on_s, fill):
         for b in range(4):
             mm(4 + b, HF, T.wq[:, 128 * b:128 * b + 128], T.wsp[:, 128 * b:128 * b + 128], T[src][:, 0:HF], T[plane][:, 0:HF], ["wq", "wsp"] + keys)
         for b in range(4):
             o, i, r, w = T[tile][:, b:640:4], bank(4 + b, HF), ["ps%d" % (4 + b)], ["%s.%d" % (tile, b)]
             if b in on_s: act(o, i, r, w, 0.03125)
             else: tsc(o, i, 0.03125, None, [A.mult], r, w)
+        fill()
         quant(T[hq][:], T[hs][:], T[tile][:], ["%s.%d" % (tile, b) for b in range(4)], [hq])
 
     def unpack(hq, hs, h):
@@ -191,41 +190,44 @@ def rank_program(g, core, T, topo):
         partner = T.cores[rank ^ STEP[k]]
         mel, mgl, mlo = ("me", "mg", 0) if k else ("lle", "llg", 40)
         ue, uf = (T.uu[:, 0:128], T.uus[:, 0:128]), (T.uu[:, 128:256], T.uus[:, 128:256])
-        for h in (0, 1): mm(4 + h, HF, *ue, T.tq[:, HF * h:HF * h + HF], T.ts[:, HF * h:HF * h + HF], ["uu", "uus", "tq"])
-        mm(6, C, *uf, T.tq[:], T.ts[:], ["uu", "uus", "tq"])
-        for b in range(4):
-            mm(b, C, T["eq%d" % b][:], T["es%d" % b][:], T.tq[:], T.ts[:], ["eq%d" % b, "tq"])
+        for h in (0, 1): mm(4 + h, HF, *ue, T.tq[:, HF * h:HF * h + HF], T.ts[:, HF * h:HF * h + HF], ["uu", "uus", "tq%d" % h])
+        mm(6, C, *uf, T.tq[:], T.ts[:], ["uu", "uus", "tq0", "tq1"])
         emit("s", lambda e: e.activation(T.sge[:, 0:HF], bank(4, HF), SG, bias=-(2.0 ** -93)), ["ps4"], ["sge0"])
         tsc(T.sge[:, HF:C], bank(5, HF), 0.0, None, [A.is_gt], ["ps5"], ["sge1"])
-        tsc(row("sgg"), bank(6, C), 0.0, None, [A.is_gt], ["ps6"], ["sgg"])
         act(row("spe"), row("sge").indirect(T.lle[:, 0:20]), ["sge0", "sge1", "lle"], ["spe"])
-        comp("spg", "sgg", "llg")
-        act(win("fw", 0), bank(0, C), ["ps0"], ["fw0"])
-        scan(T.s1[:, 0:C], row("d0"), row("sge"), A.max, ["d0", "sge0", "sge1"], ["s10"])
-        scan(T.s1[:, C:640], row("d0"), row("sgg"), A.max, ["d0", "sgg"], ["s11"])
-        tsc(T.q1[:], ends("s1", 0, 640), T.thr[:, 15:16], None, [A.is_ge], ["s10", "s11", "thr"], ["q1"])
-        tt(T.qc[:], T.q1[:], T.dd[:], A.mult, ["q1", "dd0", "dd1"], ["qc"])
-        tt(T.qd[:], T.q1[:], T.dd2[:], A.mult, ["q1", "dd2"], ["qd"])
-        tt(T.ba[:], T.pp[:], T.qc[:], A.subtract, ["pp0", "pp1", "qc"], ["ba"])
-        tt(T.cc[:], T.qd[:], T.dd[:], A.subtract, ["qd", "dd0", "dd1"], ["cc"])
 
-        def turns(i, sp, lst):
+        def turns(i, sg, sp, lst):
             c, x = slice(20 * i, 20 * i + 20), "%d" % i
+            scan(T.s1[:, C * i:C * i + C], row("d0"), row(sg), A.max, ["d0"] + ([sg] if i else [sg + "0", sg + "1"]), ["s1" + x])
+            yield
+            tsc(T.q1[:, c], ends("s1", C * i, C * i + C), T.thr[:, 15:16], None, [A.is_ge], ["s1" + x, "thr"], ["q1" + x])
+            yield
             scan(T.s2[:, C * i:C * i + C], row("d0"), row(sp), A.max, ["d0", sp], ["s2" + x])
             yield
             tsc(T.q2[:, c], ends("s2", C * i, C * i + C), T.thr[:, 15:16], None, [A.is_ge], ["s2" + x, "thr"], ["q2" + x])
             yield
-            tt(T.qm[:, c], T.q2[:, c], T.cc[:, c], A.mult, ["q2" + x, "cc"], ["qm" + x])
+            tt(T.qe[:, c], T.q2[:, c], T.q1[:, c], A.is_equal, ["q1" + x, "q2" + x], ["qe" + x])
             yield
-            tt(T.qt[:, c], T.qm[:, c], T.ba[:, c], A.add, ["qm" + x, "ba"], ["qt" + x])
+            tt(T.qm[:, c], T.qe[:, c], T.dd[:, c], A.mult, ["qe" + x, "dd" + x], ["qm" + x])
+            yield
+            tt(T.qt[:, c], T.qm[:, c], T.al[:], A.add, ["qm" + x, "al"], ["qt" + x])
             yield
             cp(T[lst][:], T.qt[:, c], ["qt" + x], [lst])
             yield
-        e, f = turns(0, "spe", "te"), turns(1, "spg", "tg")
-        for w in "eeeefef": next(e if w == "e" else f)
+        e, f = turns(0, "sge", "spe", "te"), turns(1, "sgg", "spg", "tg")
+        next(e)
+        tsc(row("sgg"), bank(6, C), 0.0, None, [A.is_gt], ["ps6"], ["sgg"])
+        comp("spg", "sgg", "llg")
+        if k == 0: unpackers()
+        for b in range(4):
+            mm(b, C, T["eq%d" % b][:], T["es%d" % b][:], T.tq[:], T.ts[:], ["eq%d" % b, "tq0", "tq1"])
+        if k == 0: comp("p1", "ngr", "lle", 20)
+        else: act(win("fw", 0), bank(0, C), ["ps0"], ["fw0"])
+        for w in "eefefefefefe": next(e if w == "e" else f)
         comp("nep", "ner", "te")
         comp("wer", "nep", mel, mlo)
-        for b in (1, 2, 3): act(win("fw", b), bank(b, C), ["ps%d" % b], ["fw%d" % b])
+        for b in (1, 2, 3) if k else (0, 1, 2, 3): act(win("fw", b), bank(b, C), ["ps%d" % b], ["fw%d" % b])
+        if k == 0: tsc(row("rr"), row("j16"), 0, None, [A.not_equal], ["j16"], ["rr"])
         compv("b1", "p1", "te")
         next(f)
         compv("b2", "b1", mel, mlo)
@@ -255,11 +257,15 @@ def rank_program(g, core, T, topo):
         for b in (0, 2, 3): act(win("gw", b), win("fw", b).indirect(T.nL[:]), ["fw%d" % b, "nL"], ["gw%d" % b])
         cp(win("gw", 1), win("fw", 1).indirect(T.nL[:]), ["fw1", "nL"], ["gw1"])
         for h in (1, 0):
-            for b in (1, 0, 2, 3):
+            def copy(b):
                 c = slice(C * b + HF * h, C * b + HF * h + HF)
                 if h: cp(T.g2[:, c], T.gw[:, c], ["gw%d" % b], ["g2%d.%d" % (b, h)])
                 else: act(T.g2[:, c], T.gw[:, c], ["gw%d" % b], ["g2%d.%d" % (b, h)])
+
+            def mean(b):
+                c = slice(C * b + HF * h, C * b + HF * h + HF)
                 tt(T.zt[:, 640 * h + b:640 * h + 640:4], win("gw", b).indirect(T.nL[:, 10 * h:10 * h + 10]), T.g2[:, c], A.add, ["gw%d" % b, "g2%d.%d" % (b, h), "nL"], ["zt%d.%d" % (h, b)])
+            for fn, b in ((copy, 1), (copy, 0), (mean, 1), (mean, 0), (copy, 2), (mean, 2), (copy, 3), (mean, 3)): fn(b)
             c = slice(HF * h, HF * h + HF)
             quant(T.zq[:, c], T.zs[:, c], T.zt[:, 640 * h:640 * h + 640], ["zt%d.%d" % (h, b) for b in range(4)], ["zq%d" % h])
             if h == 1:
@@ -275,35 +281,40 @@ def rank_program(g, core, T, topo):
         comp("wr2", "wr", "sh", 0, SH)
         comp("wt", "wr2", "te")
         comp("ngr", "b2", "tg")
-        if not last:
-            tolist("ne", "nes")
-            tolist("mg", "mgs")
-        tsc(T.hb[:], ends("mgs"), T.mod[:, 0:1], None, [A.mult], ["mgs0", "mod"], ["hb"])
+        if not last: tolist("ne", "nes")
         compm("mem", "wt", mel, mlo)
-        layer("ho", "hqo", "hso", "zq", "zs", ["zq0"], (0, 1, 2, 3))
+        layer("ho", "hqo", "hso", "zq", "zs", ["zq0"], (0, 1, 2, 3), lambda: sums("mes", "mem"))
         if not last: comp("p1", "ngr", "ne")
-        sums("mes", "mem")
+        else:
+            for i, (o, r) in enumerate((("nle", "ner"), ("nlf", "ngr"))):
+                emit("s", lambda e: e.activation(row(o), row(r), ActivationFunctionType.Identity, bias=160.0), [r], [o])
+                dma("y", T.nl[i:8:2, :], T[o][0:128:32, :], [o], [])
         tsc(T.ha[:], ends("mes"), T.mev[:, 0:1], 160.0, [A.mult, A.add], ["mes0", "mev"], ["ha"])
-        if not last: tolist("me", "mes")
-        tt(T.hc[:], T.ha[:], T.hb[:], A.add, ["ha", "hb"], ["hc"])
-        cp(T.mL[:], T.hc[:], ["hc"], ["mL"])
+        tsc(T.hb[:], ends("mgs"), T.mod[:, 0:1], None, [A.mult], ["mgs0", "mod"], ["hb"])
         unpack("hqo", "hso", 0)
-        layer("hp", "hqp", "hsp", "lq%d" % k, "ls%d" % k, ["lq%d" % k], (0, 2))
+        layer("hp", "hqp", "hsp", "lq%d" % k, "ls%d" % k, ["lq%d" % k], (0, 2), lambda: tt(T.hc[:], T.ha[:], T.hb[:], A.add, ["ha", "hb"], ["hc"]))
+        cp(T.mL[:], T.hc[:], ["hc"], ["mL"])
+        if not last:
+            tolist("mg", "mgs")
+            tolist("me", "mes")
         unpack("hqp", "hsp", 1)
-        for b in (0, 1): act(T.xst[:, b:1280:4], win("xw", b).indirect(T.mL[:]), ["xw%d.0" % b, "xw%d.1" % b, "mL"], ["xst%d" % b], 2.0)
-        for b in (2, 3): tsc(T.xst[:, b:1280:4], win("xw", b).indirect(T.mL[:]), 2.0, None, [A.mult], ["xw%d.0" % b, "xw%d.1" % b, "mL"], ["xst%d" % b])
-        quant(T.tq[:], T.ts[:], T.xst[:], ["xst%d" % b for b in range(4)], ["tq"])
+        def xs(b): return ["xw%d.0" % b, "xw%d.1" % b, "mL"]
+        for b in (0, 1): act(T.xst[:, b:1280:4], win("xw", b).indirect(T.mL[:]), xs(b), ["xst%d" % b], 2.0)
+        act(T.xst[:, 642:1280:4], win("xw", 2).indirect(T.mL[:, 10:20]), xs(2), ["xst2.1"], 2.0)
+        tsc(T.xst[:, 2:640:4], win("xw", 2).indirect(T.mL[:, 0:10]), 2.0, None, [A.mult], xs(2), ["xst2.0"])
+        tsc(T.xst[:, 3:1280:4], win("xw", 3).indirect(T.mL[:]), 2.0, None, [A.mult], xs(3), ["xst3"])
+        for h in (0, 1): quant(T.tq[:, HF * h:HF * h + HF], T.ts[:, HF * h:HF * h + HF], T.xst[:, 640 * h:640 * h + 640], ["xst0", "xst1", "xst2.%d" % h, "xst3"], ["tq%d" % h])
         if k == 0: quant(T.vq[:], T.vs[:], T.vt[:], ["vt"], ["vq"])
 
-    dma("y", T.oc[:], T.tq[:].bitcast(dt.uint8), ["tq"], [])
-    for i in range(4): dma("s", T.osc[4 * i:4 * i + 4, :], T.ts[32 * i:32 * i + 4, :], ["tq"], [])
-    mm(6, C, T.vq[:], T.vs[:], T.tq[:], T.ts[:], ["vq", "tq"])
-    tsc(T.nle[:], row("ner"), 160.0, None, [A.add], ["ner"], ["nle"])
-    cp(T.yo[:], bank(6, C), ["ps6"], ["yo"])
-    dma("y", T.nl[0:8:2, :], T.nle[0:128:32, :], ["nle"], [])
-    dma("y", T.y[:], T.yo[:], ["yo"], [])
-    tsc(T.nlf[:], row("ngr"), 160.0, None, [A.add], ["ngr"], ["nlf"])
-    dma("y", T.nl[1:8:2, :], T.nlf[0:128:32, :], ["nlf"], [])
+    for h in (0, 1):
+        c = slice(HF * h, HF * h + HF)
+        mm(6 + h, HF, T.vq[:], T.vs[:], T.tq[:, c], T.ts[:, c], ["vq", "tq%d" % h])
+    cp(T.yo[:, 0:HF], bank(6, HF), ["ps6"], ["yo0"])
+    act(T.yo[:, HF:C], bank(7, HF), ["ps7"], ["yo1"])
+    dma("y", T.oc[:], T.tq[:].bitcast(dt.uint8), ["tq0", "tq1"], [])
+    dma("y", T.y[:, 0:HF], T.yo[:, 0:HF], ["yo0"], [])
+    dma("s", T.y[:, HF:C], T.yo[:, HF:C], ["yo1"], [])
+    for i in range(4): dma("y" if i < 2 else "s", T.osc[4 * i:4 * i + 4, :], T.ts[32 * i:32 * i + 4, :], ["tq0", "tq1"], [])
     for i in range(ndma[0]): need("g", ("x", "dm%d" % i, 16, {}))
     for s, n in cnt.items(): need("g", ("x", s, n, {}))
     for k in range(ROUNDS):

@@ -14,7 +14,7 @@ def _scratch():
         for k, n in kw.items():
             s[k] = ("sbuf", [128, n], dtype)
     sb(BF, xin=1280, xst=1280, zt=1280, ho=640, hp=640, ut=512, vt=512, et=516, fw=1280, gw=1280, g2=1280, xw=1280)
-    sb(BF, idr=C, mk=C, rr=C, d0=C, thr=C, j16=C)
+    sb(BF, idr=C, mk=C, mke=C, rr=C, d0=C, thr=C, j16=C)
     sb(BF, ner=C, ngr=C, p1=C, sge=C, sgg=C, spe=C, spg=C, s1=640, s2=640, nep=C, wer=C, b1=C, b2=C)
     sb(BF, alm=C, ngm=C, as_=640, rw=C, nem=C, nes=C, tgr=C, wr=C, wr2=C, wt=C, mgm=C, mgs=C, mem=C, mes=C)
     sb(F32, yo=C, nlf=C, nle=C, al=20, dd=40, ef=60, gf=60, t1=60, t2=60, mev=2, mod=2, pmf=2)
@@ -107,8 +107,8 @@ def rank_program(g, core, T, topo):
     def compv(out, w, lst, lo=0):
         cp(row(out), row(w).indirect(T[lst][:, lo:lo + 20]), [w, lst], [out])
 
-    def compm(out, w, lst, lo=0, key=None):
-        tt(row(out), row(w).indirect(T[lst][:, lo:lo + 20]), row("mk"), A.mult, [w, "mk"] + (key or [lst]), [out])
+    def compm(out, w, lst, lo=0, key=None, mask="mk"):
+        tt(row(out), row(w).indirect(T[lst][:, lo:lo + 20]), row(mask), A.mult, [w, mask] + (key or [lst]), [out])
 
     def sums(sc, x, lo=0): scan(T[sc][:, lo:lo + C], row("rr"), row(x), A.add, ["rr", x], [sc + "%d" % lo])
     def tolist(l, sc): tsc(T[l][:], ends(sc), 160.0, None, [A.add], [sc + "0"], [l])
@@ -168,23 +168,34 @@ def rank_program(g, core, T, topo):
         for b in range(4):
             quant(T["eq%d" % b][:], T["es%d" % b][:], T.et[:, 3 - b:515 - b], ["et"], ["eq%d" % b])
 
-    def layer(tile, hq, hs, src, plane, keys, on_s, fill):
+    def layer(tile, h, b0):
+        c = slice(HF * h, HF * h + HF)
         for b in range(4):
-            mm(4 + b, HF, T.wq[:, 128 * b:128 * b + 128], T.wsp[:, 128 * b:128 * b + 128], T[src][:, 0:HF], T[plane][:, 0:HF], ["wq", "wsp"] + keys)
+            mm(b0 + b, HF, T.wq[:, 128 * b:128 * b + 128], T.wsp[:, 128 * b:128 * b + 128], T.zq[:, c], T.zs[:, c], ["wq", "wsp", "zq%d" % h])
         for b in range(4):
-            o, i, r, w = T[tile][:, b:640:4], bank(4 + b, HF), ["ps%d" % (4 + b)], ["%s.%d" % (tile, b)]
-            if b in on_s: act(o, i, r, w, 0.03125)
-            else: tsc(o, i, 0.03125, None, [A.mult], r, w)
-        fill()
-        quant(T[hq][:], T[hs][:], T[tile][:], ["%s.%d" % (tile, b) for b in range(4)], [hq])
+            act(T[tile][:, b:640:4], bank(b0 + b, HF), ["ps%d" % (b0 + b)], ["%s.%d" % (tile, b)], 0.03125)
 
-    def unpack(hq, hs, h):
+    def pack(tile, hq, hs): quant(T[hq][:], T[hs][:], T[tile][:], ["%s.%d" % (tile, b) for b in range(4)], [hq])
+
+    def unpack(hq, hs, h, b0):
         for b in range(4):
-            mm(b, HF, T["eq%d" % b][:], T["es%d" % b][:], T[hq][:], T[hs][:], ["eq%d" % b, hq])
+            mm(b0 + b, HF, T["eq%d" % b][:], T["es%d" % b][:], T[hq][:], T[hs][:], ["eq%d" % b, hq])
         for b in range(4):
             c = slice(C * b + HF * h, C * b + HF * h + HF)
-            tt(T.xw[:, c], T.gw[:, c], bank(b, HF), A.add, ["gw%d" % b, "ps%d" % b], ["xw%d.%d" % (b, h)])
+            tt(T.xw[:, c], T.gw[:, c], bank(b0 + b, HF), A.add, ["gw%d" % b, "ps%d" % (b0 + b)], ["xw%d.%d" % (b, h)])
 
+    def send(k, partner):
+        rid, pid, _ = topo.addr(partner)
+        m, n = topo.mask(core, partner), 2 * len(topo.engines(core, partner))
+        order("g", "remote", ["hqp"], [])
+        arr, loc = T.sem["arr%d" % k], T.sem["loc%d" % k]
+        g.remote_dma(T["lq%d" % k][:].bitcast(dt.uint8), T.hqp[:].bitcast(dt.uint8), arr, loc, pid, rid, m)
+        g.remote_dma(T["ls%d" % k][:], T.hsp[:], arr, loc, pid, rid, m)
+        note(("remote", "loc%d" % k, n, {}), ["hqp"], [])
+        note(("remote", "arr%d" % k, n, {}), [], ["lq%d" % k])
+        moved.append((k, n))
+
+    moved = []
     for k in range(ROUNDS):
         last = k == ROUNDS - 1
         partner = T.cores[rank ^ STEP[k]]
@@ -227,7 +238,9 @@ def rank_program(g, core, T, topo):
         comp("nep", "ner", "te")
         comp("wer", "nep", mel, mlo)
         for b in (1, 2, 3) if k else (0, 1, 2, 3): act(win("fw", b), bank(b, C), ["ps%d" % b], ["fw%d" % b])
-        if k == 0: tsc(row("rr"), row("j16"), 0, None, [A.not_equal], ["j16"], ["rr"])
+        if k == 0:
+            tsc(row("rr"), row("j16"), 0, None, [A.not_equal], ["j16"], ["rr"])
+            tsc(row("mke"), row("mk"), T.mev[:, 0:1], None, [A.mult], ["mk", "mev"], ["mke"])
         compv("b1", "p1", "te")
         next(f)
         compv("b2", "b1", mel, mlo)
@@ -246,14 +259,17 @@ def rank_program(g, core, T, topo):
         comp("ner", "rw", "sh", 0, SH)
         comp("wr", "idr", "sh", 20, SH)
         tsc(T.aL[:], ends("as_"), 160.0, None, [A.add], ["as_0"], ["aL"])
-        tsc(T.fz[:], ends("as_", C, 640), T.mod[:, 0:1], None, [A.mult], ["as_%d" % C, "mod"], ["fz"])
+        tsc(T.fz[:], ends("as_", C, 640), T.mod[:, 0:1], 160.0, [A.mult, A.add], ["as_%d" % C, "mod"], ["fz"])
         compm("mgm", "tgr", "aL")
-        compm("nem", "rw", "sh", 0, SH)
+        compm("nem", "rw", "sh", 0, SH, "mke")
         sums("mgs", "mgm")
         sums("nes", "nem")
-        tsc(T.fa[:], ends("nes"), T.mev[:, 0:1], 160.0, [A.mult, A.add], ["nes0", "mev"], ["fa"])
-        tt(T.fb[:], T.fa[:], T.fz[:], A.add, ["fa", "fz"], ["fb"])
+        tt(T.fb[:], ends("nes"), T.fz[:], A.add, ["nes0", "fz"], ["fb"])
         cp(T.nL[:], T.fb[:], ["fb"], ["nL"])
+        if not last:
+            cp(T.ne[:], T.fb[:], ["fb"], ["ne"])
+            for a in range(4): dma("y", T.ne[32 * a + 16:32 * a + 32, :], T.nL[32 * a:32 * a + 16, :], ["nL", "ne"], ["ne%d" % a])
+        NE = ["ne"] + ["ne%d" % a for a in range(4)]
         for b in (0, 2, 3): act(win("gw", b), win("fw", b).indirect(T.nL[:]), ["fw%d" % b, "nL"], ["gw%d" % b])
         cp(win("gw", 1), win("fw", 1).indirect(T.nL[:]), ["fw1", "nL"], ["gw1"])
         for h in (1, 0):
@@ -265,39 +281,37 @@ def rank_program(g, core, T, topo):
             def mean(b):
                 c = slice(C * b + HF * h, C * b + HF * h + HF)
                 tt(T.zt[:, 640 * h + b:640 * h + 640:4], win("gw", b).indirect(T.nL[:, 10 * h:10 * h + 10]), T.g2[:, c], A.add, ["gw%d" % b, "g2%d.%d" % (b, h), "nL"], ["zt%d.%d" % (h, b)])
-            for fn, b in ((copy, 1), (copy, 0), (mean, 1), (mean, 0), (copy, 2), (mean, 2), (copy, 3), (mean, 3)): fn(b)
+            if h:
+                for fn, b in ((copy, 1), (copy, 0), (mean, 1), (mean, 0), (copy, 2), (mean, 2), (copy, 3), (mean, 3)): fn(b)
+            else:
+                for b in range(4): copy(b)
+                comp("wr2", "wr", "sh", 0, SH)
+                layer("hp", 1, 4)
+                for b in range(4): mean(b)
+                pack("hp", "hqp", "hsp")
             c = slice(HF * h, HF * h + HF)
             quant(T.zq[:, c], T.zs[:, c], T.zt[:, 640 * h:640 * h + 640], ["zt%d.%d" % (h, b) for b in range(4)], ["zq%d" % h])
-            if h == 1:
-                rid, pid, _ = topo.addr(partner)
-                eng = topo.engines(core, partner)
-                lo, hi = sum(1 << i for i in eng[:8]), sum(1 << i for i in eng[-8:])
-                order("g", "remote", ["zq1"], [])
-                lq, ls, arr, loc = T["lq%d" % k], T["ls%d" % k], T.sem["arr%d" % k], T.sem["loc%d" % k]
-                g.remote_dma(lq[:].bitcast(dt.uint8), T.zq[:, c].bitcast(dt.uint8), arr, loc, pid, rid, lo)
-                g.remote_dma(ls[:], T.zs[:, c], arr, loc, pid, rid, hi)
-                note(("remote", "loc%d" % k, 16, {}), ["zq1"], [])
-                note(("remote", "arr%d" % k, 16, {}), [], ["lq%d" % k])
-        comp("wr2", "wr", "sh", 0, SH)
+        send(k, partner)
         comp("wt", "wr2", "te")
-        comp("ngr", "b2", "tg")
-        if not last: tolist("ne", "nes")
         compm("mem", "wt", mel, mlo)
-        layer("ho", "hqo", "hso", "zq", "zs", ["zq0"], (0, 1, 2, 3), lambda: sums("mes", "mem"))
-        if not last: comp("p1", "ngr", "ne")
+        layer("ho", 0, 0)
+        sums("mes", "mem")
+        pack("ho", "hqo", "hso")
+        comp("ngr", "b2", "tg")
+        if not last: comp("p1", "ngr", "ne", 0, NE)
         else:
             for i, (o, r) in enumerate((("nle", "ner"), ("nlf", "ngr"))):
                 emit("s", lambda e: e.activation(row(o), row(r), ActivationFunctionType.Identity, bias=160.0), [r], [o])
                 dma("y", T.nl[i:8:2, :], T[o][0:128:32, :], [o], [])
         tsc(T.ha[:], ends("mes"), T.mev[:, 0:1], 160.0, [A.mult, A.add], ["mes0", "mev"], ["ha"])
         tsc(T.hb[:], ends("mgs"), T.mod[:, 0:1], None, [A.mult], ["mgs0", "mod"], ["hb"])
-        unpack("hqo", "hso", 0)
-        layer("hp", "hqp", "hsp", "lq%d" % k, "ls%d" % k, ["lq%d" % k], (0, 2), lambda: tt(T.hc[:], T.ha[:], T.hb[:], A.add, ["ha", "hb"], ["hc"]))
+        tt(T.hc[:], T.ha[:], T.hb[:], A.add, ["ha", "hb"], ["hc"])
+        unpack("hqo", "hso", 0, 4)
         cp(T.mL[:], T.hc[:], ["hc"], ["mL"])
         if not last:
             tolist("mg", "mgs")
             tolist("me", "mes")
-        unpack("hqp", "hsp", 1)
+        unpack("lq%d" % k, "ls%d" % k, 1, 0)
         def xs(b): return ["xw%d.0" % b, "xw%d.1" % b, "mL"]
         for b in (0, 1): act(T.xst[:, b:1280:4], win("xw", b).indirect(T.mL[:]), xs(b), ["xst%d" % b], 2.0)
         act(T.xst[:, 642:1280:4], win("xw", 2).indirect(T.mL[:, 10:20]), xs(2), ["xst2.1"], 2.0)
@@ -317,6 +331,6 @@ def rank_program(g, core, T, topo):
     for i in range(4): dma("y" if i < 2 else "s", T.osc[4 * i:4 * i + 4, :], T.ts[32 * i:32 * i + 4, :], ["tq0", "tq1"], [])
     for i in range(ndma[0]): need("g", ("x", "dm%d" % i, 16, {}))
     for s, n in cnt.items(): need("g", ("x", s, n, {}))
-    for k in range(ROUNDS):
-        need("g", ("x", "loc%d" % k, 16, {}))
-        need("g", ("x", "arr%d" % k, 16, {}))
+    for k, n in moved:
+        need("g", ("x", "loc%d" % k, n, {}))
+        need("g", ("x", "arr%d" % k, n, {}))

from concourse.mybir import dt, AluOpType, ActivationFunctionType
import comms_topo

C, HF = 320, 160
ROUNDS = 3
STEP = [1, 2, 4]
BF, F32, I32, U16, U8, MXC = "bfloat16", "float32", "int32", "uint16", "uint8", "float8_e4m3fn_x4"


def _scratch():
    s = {}

    def sb(dtype, **kw):
        for k, n in kw.items():
            s[k] = ("sbuf", [128, n], dtype)
    sb(BF, xin=1280, xst=1280, zt=1280, ho=640, hp=640, ut=512, vt=512, et=516, fw=1280, gw=1280, g2=1280, xw=1280)
    sb(BF, idr=C, mk=C, mke=C, rr=C, d0=C, thr=C, j16=C)
    sb(BF, ner=C, ngr=C, p1=C, sge=C, sgg=C, spe=C, spg=C, s1=640, s2=640, nep=C, wer=C, b1=C, b2=C)
    sb(BF, alm=C, ngm=C, as_=640, rw=C, nem=C, nes=C, tgr=C, wr=C, wr2=C, wt=C, mgm=C, mgs=C, mem=C, mes=C)
    sb(F32, yo=C, nlf=C, nle=C, al=20, dd=40, ef=60, gf=60, t1=60, t2=60, mev=2, mod=2, pmf=2)
    sb(F32, q1=40, qe=40, q2=40, qm=40, qt=40, fa=20, fb=20, fz=20, ha=20, hb=20, hc=20)
    sb(I32, own=60, shd=60, upd=60, jp=C, pc=2, pa=2, pb=2, ai=20, ui=16)
    sb(U16, lle=60, llg=60, ne=20, me=20, mg=20, te=20, tg=20, aL=20, sh=40, nL=20, mL=20, ul=16)
    sb(MXC, tq=C, zq=C, hqo=HF, hqp=HF, uq=128, uu=256, vq=128, wq=512, eq0=128, eq1=128, eq2=128, eq3=128)
    sb(U8, ts=C, zs=C, hso=HF, hsp=HF, us=128, uus=256, vs=128, wsp=512, es0=128, es1=128, es2=128, es3=128)
    for k in range(ROUNDS):
        s["lq%d" % k] = ("sbuf", [128, HF], MXC)
        s["ls%d" % k] = ("sbuf", [128, HF], U8)
    s["ps"] = ("psum", [128, 512 * 8], F32)
    return s


SCRATCH = _scratch()
SEMAPHORES = ["qv", "qs", "qp", "qg"] + ["arr%d" % k for k in range(ROUNDS)] + ["loc%d" % k for k in range(ROUNDS)] + ["dm%d" % k for k in range(48)]


def rank_program(g, core, T, topo):
    rank = T.rank_of(core)
    if rank is None:
        return
    A = AluOpType
    CP, SG = ActivationFunctionType.Copy, ActivationFunctionType.Sign
    V, S, P = g.vector, g.scalar, g.tensor
    queue = {"v": V, "s": S, "p": P, "g": g, "y": g.sync}
    semof = {"v": "qv", "s": "qs", "p": "qp", "g": "qg"}
    cnt = {}
    known = {q: {} for q in queue}
    writer, readers, ndma = {}, {}, [0]

    def need(q, tok):
        if known[q].get(tok[1], 0) < tok[2]:
            queue[q].wait_ge(T.sem[tok[1]], tok[2])
            known[q][tok[1]] = tok[2]
        for k, n in tok[3].items():
            if known[q].get(k, 0) < n: known[q][k] = n

    def order(q, who, reads, writes):
        toks = []
        for k in reads:
            if k in writer: toks.append(writer[k])
            if k[:2] == "ps": toks += [t for t in readers.get(k, []) if t[0] != who]
        for k in writes:
            if k in writer and writer[k][0] != who: toks.append(writer[k])
            toks += [t for t in readers.get(k, []) if t[0] != who]
        for t in sorted(toks, key=lambda t: -t[2]): need(q, t)

    def note(tok, reads, writes):
        for k in reads: readers.setdefault(k, []).append(tok)
        for k in writes:
            writer[k] = tok
            readers[k] = []

    def emit(q, fn, reads, writes):
        order(q, q, reads, writes)
        s = semof[q]
        cnt[s] = cnt.get(s, 0) + 1
        fn(queue[q]).then_inc(T.sem[s], 1)
        note((q, s, cnt[s], dict(known[q])), reads, writes)

    def dma(q, out, in_, reads, writes):
        s = "dm%d" % ndma[0]
        ndma[0] += 1
        order(q, s, reads, writes)
        queue[q].dma_start(out, in_).then_inc(T.sem[s], 16)
        note((s, s, 16, dict(known[q])), reads, writes)

    def vv(fn, r, w): emit("v", fn, r, w)
    def gg(fn, r, w): emit("g", fn, r, w)
    def tt(out, in0, in1, op, r, w): vv(lambda e: e.tensor_tensor(out, in0, in1, op), r, w)
    def tsc(out, in0, s1, s2, ops, r, w): vv(lambda e: e.tensor_scalar(out, in0, s1, s2, *ops), r, w)
    def cp(out, in_, r, w): vv(lambda e: e.tensor_copy(out, in_), r, w)
    def act(out, in_, r, w, scale=1.0): emit("s", lambda e: e.activation(out, in_, CP) if scale == 1.0 else e.activation(out, in_, CP, scale=scale), r, w)
    def quant(c, s, t, r, w): vv(lambda e: e.quantize_mx(c, s, t), r, w)
    def scan(out, d, x, op, r, w): vv(lambda e: e.tensor_tensor_scan(out, d, x, 0.0, A.mult, op), r, w)

    def mm(bank, n, a, sa, b, sb, r):
        emit("p", lambda e: e.matmul_mx(T.ps[:, 512 * bank:512 * bank + n], a, sa, b, sb, True, True), r, ["ps%d" % bank])

    def bank(i, n): return T.ps[:, 512 * i:512 * i + n]
    def win(name, b): return T[name][:, C * b:C * b + C]
    def row(name): return T[name][:]
    def ends(name, lo=0, hi=C): return T[name][:, lo + 15:hi:16]

    def comp(out, w, lst, lo=0, key=None):
        act(row(out), row(w).indirect(T[lst][:, lo:lo + 20]), [w] + (key or [lst]), [out])

    def compv(out, w, lst, lo=0):
        cp(row(out), row(w).indirect(T[lst][:, lo:lo + 20]), [w, lst], [out])

    def compm(out, w, lst, lo=0, key=None, mask="mk"):
        tt(row(out), row(w).indirect(T[lst][:, lo:lo + 20]), row(mask), A.mult, [w, mask] + (key or [lst]), [out])

    def sums(sc, x, lo=0): scan(T[sc][:, lo:lo + C], row("rr"), row(x), A.add, ["rr", x], [sc + "%d" % lo])
    def tolist(l, sc): tsc(T[l][:], ends(sc), 160.0, None, [A.add], [sc + "0"], [l])

    vv(lambda e: e.memset(T.shd[:], 0), [], ["shd"])
    vv(lambda e: e.memset(T.upd[:], 0), [], ["upd"])
    vv(lambda e: e.memset(T.et[:], 0.5), [], ["et"])
    dma("y", T.ut[:], T.u[:], [], ["ut"])
    dma("y", T.xin[:, 0:640], T.x[:, 0:640], [], ["xin0"])
    lists = (T.pr, T.nx, T.iv)
    for i, src in enumerate(lists): dma("s", T.own[:, 20 * i:20 * i + 20], src[:], [], ["own%d" % i])
    for i, src in enumerate(lists): dma("s", T.shd[16:128, 20 * i:20 * i + 20], src[0:112, :], ["shd"], ["shd%d" % i])
    for i, src in enumerate(lists): dma("s", T.upd[0:112, 20 * i:20 * i + 20], src[16:128, :], ["upd"], ["upd%d" % i])
    dma("y", T.xin[:, 640:1280], T.x[:, 640:1280], [], ["xin1"])
    dma("y", T.wq[:].bitcast(dt.uint8), T.wc[:], [], ["wq"])
    dma("y", T.wsp[:], T.ws[:], [], ["wsp"])
    dma("y", T.vt[:], T.v[:], [], ["vt"])

    gg(lambda e: e.iota(T.pc[:, 0:1], [[0, 1]], 0, 1), [], ["pc"])
    gg(lambda e: e.iota(T.ui[:], [[16, 2], [32, 4], [0, 2]], 0, 0), [], ["ui"])
    gg(lambda e: e.iota(T.ai[:], [[16, 20]], 0, 0), [], ["ai"])
    gg(lambda e: e.iota(T.jp[:], [[1, C]], 128, -1), [], ["jp"])
    gg(lambda e: e.iota(T.idr[:], [[1, C]], -160, 0, allow_small_or_imprecise_dtypes=True), [], ["idr"])
    gg(lambda e: e.affine_select(T.et[:], T.et[:], [[-1, 516]], A.is_equal, 0.0, 3, 4), ["et"], ["et"])
    gg(lambda e: e.iota(T.j16[:], [[0, 20], [1, 16]], 0, 0, allow_small_or_imprecise_dtypes=True), [], ["j16"])
    tsc(T.pa[:, 0:1], T.pc[:, 0:1], 15, None, [A.bitwise_and], ["pc"], ["pa"])
    tsc(T.pb[:, 0:1], T.pc[:, 0:1], 31, None, [A.bitwise_and], ["pc"], ["pb"])
    cp(T.ul[:], T.ui[:], ["ui"], ["ul"])
    cp(T.pmf[:, 0:1], T.pa[:, 0:1], ["pa"], ["pmf"])
    tsc(T.mev[:, 0:1], T.pb[:, 0:1], 16, None, [A.is_lt], ["pb"], ["mev"])
    tsc(T.mod[:, 0:1], T.pb[:, 0:1], 16, None, [A.is_ge], ["pb"], ["mod"])
    tsc(T.al[:], T.ai[:], T.pmf[:, 0:1], None, [A.add], ["ai", "pmf"], ["al"])
    tsc(T.jp[:], T.jp[:], 15, None, [A.bitwise_and], ["jp"], ["jp"])
    tsc(row("mk"), T.jp[:], 0, None, [A.is_equal], ["jp"], ["mk"])
    tsc(row("d0"), row("mk"), -2.0, 2.0, [A.mult, A.add], ["mk"], ["d0"])
    ow, sh, up = ["own0", "own1", "own2"], ["shd0", "shd1", "shd2"], ["upd0", "upd1", "upd2"]
    tt(T.t1[:], T.own[:], T.shd[:], A.subtract, ow + sh, ["t1"])
    tt(T.t2[:], T.upd[:], T.own[:], A.subtract, ow + up, ["t2"])
    tsc(T.t1[:], T.t1[:], T.mev[:, 0:1], None, [A.mult], ["t1", "mev"], ["t1"])
    tsc(T.t2[:], T.t2[:], T.mev[:, 0:1], None, [A.mult], ["t2", "mev"], ["t2"])
    tt(T.ef[:], T.t1[:], T.shd[:], A.add, ["t1"] + sh, ["ef"])
    tt(T.gf[:], T.t2[:], T.own[:], A.add, ["t2"] + ow, ["gf"])
    cp(T.lle[:], T.ef[:], ["ef"], ["lle"])
    cp(T.llg[:], T.gf[:], ["gf"], ["llg"])
    comp("ner", "idr", "lle", 20)
    quant(T.uq[:], T.us[:], T.ut[:], ["ut"], ["uq"])
    cp(T.uu[:].bitcast(dt.uint32), T.uq[:].bitcast(dt.uint32).indirect(T.ul[:]), ["uq", "ul"], ["uu"])
    act(T.uus[:], T.us[:].indirect(T.ul[:]), ["uq", "ul"], ["uus"])
    for h in (0, 1): quant(T.tq[:, HF * h:HF * h + HF], T.ts[:, HF * h:HF * h + HF], T.xin[:, 640 * h:640 * h + 640], ["xin%d" % h], ["tq%d" % h])
    scan(row("thr"), row("d0"), row("mk"), A.max, ["d0", "mk"], ["thr"])
    for i, (f, l) in enumerate((("ef", "lle"), ("gf", "llg"))):
        c = slice(20 * i, 20 * i + 20)
        tt(T.dd[:, c], T[f][:, 0:20], T.al[:], A.subtract, [f, "al"], ["dd%d" % i])
    comp("ngr", "idr", "llg", 20)

    def unpackers():
        for b in range(4):
            quant(T["eq%d" % b][:], T["es%d" % b][:], T.et[:, 3 - b:515 - b], ["et"], ["eq%d" % b])

    def layer(tile, h, b0):
        c = slice(HF * h, HF * h + HF)
        for b in range(4):
            mm(b0 + b, HF, T.wq[:, 128 * b:128 * b + 128], T.wsp[:, 128 * b:128 * b + 128], T.zq[:, c], T.zs[:, c], ["wq", "wsp", "zq%d" % h])
        for b in range(4):
            act(T[tile][:, b:640:4], bank(b0 + b, HF), ["ps%d" % (b0 + b)], ["%s.%d" % (tile, b)], 0.03125)

    def pack(tile, hq, hs): quant(T[hq][:], T[hs][:], T[tile][:], ["%s.%d" % (tile, b) for b in range(4)], [hq])

    def unpack(hq, hs, h, b0):
        for b in range(4):
            mm(b0 + b, HF, T["eq%d" % b][:], T["es%d" % b][:], T[hq][:], T[hs][:], ["eq%d" % b, hq])
        for b in range(4):
            c = slice(C * b + HF * h, C * b + HF * h + HF)
            tt(T.xw[:, c], T.gw[:, c], bank(b0 + b, HF), A.add, ["gw%d" % b, "ps%d" % (b0 + b)], ["xw%d.%d" % (b, h)])

    def send(k, partner):
        rid, pid, _ = topo.addr(partner)
        m, n = topo.mask(core, partner), 2 * len(topo.engines(core, partner))
        order("g", "remote", ["hqp"], [])
        arr, loc = T.sem["arr%d" % k], T.sem["loc%d" % k]
        g.remote_dma(T["lq%d" % k][:].bitcast(dt.uint8), T.hqp[:].bitcast(dt.uint8), arr, loc, pid, rid, m)
        g.remote_dma(T["ls%d" % k][:], T.hsp[:], arr, loc, pid, rid, m)
        note(("remote", "loc%d" % k, n, {}), ["hqp"], [])
        note(("remote", "arr%d" % k, n, {}), [], ["lq%d" % k])
        moved.append((k, n))

    moved = []
    for k in range(ROUNDS):
        last = k == ROUNDS - 1
        partner = T.cores[rank ^ STEP[k]]
        mel, mgl, mlo = ("me", "mg", 0) if k else ("lle", "llg", 40)
        ue, uf = (T.uu[:, 0:128], T.uus[:, 0:128]), (T.uu[:, 128:256], T.uus[:, 128:256])
        for h in (0, 1): mm(4 + h, HF, *ue, T.tq[:, HF * h:HF * h + HF], T.ts[:, HF * h:HF * h + HF], ["uu", "uus", "tq%d" % h])
        mm(6, C, *uf, T.tq[:], T.ts[:], ["uu", "uus", "tq0", "tq1"])
        emit("s", lambda e: e.activation(T.sge[:, 0:HF], bank(4, HF), SG, bias=-(2.0 ** -93)), ["ps4"], ["sge0"])
        tsc(T.sge[:, HF:C], bank(5, HF), 0.0, None, [A.is_gt], ["ps5"], ["sge1"])
        act(row("spe"), row("sge").indirect(T.lle[:, 0:20]), ["sge0", "sge1", "lle"], ["spe"])

        def turns(i, sg, sp, lst):
            c, x = slice(20 * i, 20 * i + 20), "%d" % i
            scan(T.s1[:, C * i:C * i + C], row("d0"), row(sg), A.max, ["d0"] + ([sg] if i else [sg + "0", sg + "1"]), ["s1" + x])
            yield
            tsc(T.q1[:, c], ends("s1", C * i, C * i + C), T.thr[:, 15:16], None, [A.is_ge], ["s1" + x, "thr"], ["q1" + x])
            yield
            scan(T.s2[:, C * i:C * i + C], row("d0"), row(sp), A.max, ["d0", sp], ["s2" + x])
            yield
            tsc(T.q2[:, c], ends("s2", C * i, C * i + C), T.thr[:, 15:16], None, [A.is_ge], ["s2" + x, "thr"], ["q2" + x])
            yield
            tt(T.qe[:, c], T.q2[:, c], T.q1[:, c], A.is_equal, ["q1" + x, "q2" + x], ["qe" + x])
            yield
            tt(T.qm[:, c], T.qe[:, c], T.dd[:, c], A.mult, ["qe" + x, "dd" + x], ["qm" + x])
            yield
            tt(T.qt[:, c], T.qm[:, c], T.al[:], A.add, ["qm" + x, "al"], ["qt" + x])
            yield
            cp(T[lst][:], T.qt[:, c], ["qt" + x], [lst])
            yield
        e, f = turns(0, "sge", "spe", "te"), turns(1, "sgg", "spg", "tg")
        next(e)
        tsc(row("sgg"), bank(6, C), 0.0, None, [A.is_gt], ["ps6"], ["sgg"])
        comp("spg", "sgg", "llg")
        if k == 0: unpackers()
        for b in range(4):
            mm(b, C, T["eq%d" % b][:], T["es%d" % b][:], T.tq[:], T.ts[:], ["eq%d" % b, "tq0", "tq1"])
        if k == 0: comp("p1", "ngr", "lle", 20)
        else: act(win("fw", 0), bank(0, C), ["ps0"], ["fw0"])
        for w in "eefefefefefe": next(e if w == "e" else f)
        comp("nep", "ner", "te")
        comp("wer", "nep", mel, mlo)
        for b in (1, 2, 3) if k else (0, 1, 2, 3): act(win("fw", b), bank(b, C), ["ps%d" % b], ["fw%d" % b])
        if k == 0:
            tsc(row("rr"), row("j16"), 0, None, [A.not_equal], ["j16"], ["rr"])
            tsc(row("mke"), row("mk"), T.mev[:, 0:1], None, [A.mult], ["mk", "mev"], ["mke"])
        compv("b1", "p1", "te")
        next(f)
        compv("b2", "b1", mel, mlo)
        next(f)
        next(f)
        compm("alm", "wer", mgl, mlo)
        compm("ngm", "b2", "tg")
        sums("as_", "alm", 0)
        sums("as_", "ngm", C)
        for a in range(4):
            c = 32 * ((a + 1) % 4)
            tsc(T.sh[c:c + 32, :], T.as_[32 * a:32 * a + 32, 15:640:16], 160.0, None, [A.add], ["as_0", "as_%d" % C], ["sh%d" % a])
        SH = ["sh%d" % a for a in range(4)]
        comp("tgr", "idr", "tg")
        comp("rw", "nep", "sh", 20, SH)
        comp("ner", "rw", "sh", 0, SH)
        comp("wr", "idr", "sh", 20, SH)
        tsc(T.aL[:], ends("as_"), 160.0, None, [A.add], ["as_0"], ["aL"])
        tsc(T.fz[:], ends("as_", C, 640), T.mod[:, 0:1], 160.0, [A.mult, A.add], ["as_%d" % C, "mod"], ["fz"])
        compm("mgm", "tgr", "aL")
        compm("nem", "rw", "sh", 0, SH, "mke")
        sums("mgs", "mgm")
        sums("nes", "nem")
        tt(T.fb[:], ends("nes"), T.fz[:], A.add, ["nes0", "fz"], ["fb"])
        cp(T.nL[:], T.fb[:], ["fb"], ["nL"])
        if not last:
            cp(T.ne[:], T.fb[:], ["fb"], ["ne"])
            for a in range(4): dma("y", T.ne[32 * a + 16:32 * a + 32, :], T.nL[32 * a:32 * a + 16, :], ["nL", "ne"], ["ne%d" % a])
        NE = ["ne"] + ["ne%d" % a for a in range(4)]
        for b in (0, 2, 3): act(win("gw", b), win("fw", b).indirect(T.nL[:]), ["fw%d" % b, "nL"], ["gw%d" % b])
        cp(win("gw", 1), win("fw", 1).indirect(T.nL[:]), ["fw1", "nL"], ["gw1"])
        for h in (1, 0):
            def copy(b):
                c = slice(C * b + HF * h, C * b + HF * h + HF)
                if h: cp(T.g2[:, c], T.gw[:, c], ["gw%d" % b], ["g2%d.%d" % (b, h)])
                else: act(T.g2[:, c], T.gw[:, c], ["gw%d" % b], ["g2%d.%d" % (b, h)])

            def mean(b):
                c = slice(C * b + HF * h, C * b + HF * h + HF)
                tt(T.zt[:, 640 * h + b:640 * h + 640:4], win("gw", b).indirect(T.nL[:, 10 * h:10 * h + 10]), T.g2[:, c], A.add, ["gw%d" % b, "g2%d.%d" % (b, h), "nL"], ["zt%d.%d" % (h, b)])
            if h:
                for fn, b in ((copy, 1), (copy, 0), (mean, 1), (mean, 0), (copy, 2), (mean, 2), (copy, 3), (mean, 3)): fn(b)
            else:
                for b in range(4): copy(b)
                comp("wr2", "wr", "sh", 0, SH)
                layer("hp", 1, 4)
                for b in range(4): mean(b)
                pack("hp", "hqp", "hsp")
            c = slice(HF * h, HF * h + HF)
            quant(T.zq[:, c], T.zs[:, c], T.zt[:, 640 * h:640 * h + 640], ["zt%d.%d" % (h, b) for b in range(4)], ["zq%d" % h])
        send(k, partner)
        comp("wt", "wr2", "te")
        compm("mem", "wt", mel, mlo)
        layer("ho", 0, 0)
        sums("mes", "mem")
        pack("ho", "hqo", "hso")
        comp("ngr", "b2", "tg")
        if not last: comp("p1", "ngr", "ne", 0, NE)
        else:
            for i, (o, r) in enumerate((("nle", "ner"), ("nlf", "ngr"))):
                emit("s", lambda e: e.activation(row(o), row(r), ActivationFunctionType.Identity, bias=160.0), [r], [o])
                dma("y", T.nl[i:8:2, :], T[o][0:128:32, :], [o], [])
        tsc(T.ha[:], ends("mes"), T.mev[:, 0:1], 160.0, [A.mult, A.add], ["mes0", "mev"], ["ha"])
        tsc(T.hb[:], ends("mgs"), T.mod[:, 0:1], None, [A.mult], ["mgs0", "mod"], ["hb"])
        tt(T.hc[:], T.ha[:], T.hb[:], A.add, ["ha", "hb"], ["hc"])
        unpack("hqo", "hso", 0, 4)
        cp(T.mL[:], T.hc[:], ["hc"], ["mL"])
        if not last:
            tolist("mg", "mgs")
            tolist("me", "mes")
        unpack("lq%d" % k, "ls%d" % k, 1, 0)
        def xs(b): return ["xw%d.0" % b, "xw%d.1" % b, "mL"]
        for b in (0, 1): act(T.xst[:, b:1280:4], win("xw", b).indirect(T.mL[:]), xs(b), ["xst%d" % b], 2.0)
        act(T.xst[:, 642:1280:4], win("xw", 2).indirect(T.mL[:, 10:20]), xs(2), ["xst2.1"], 2.0)
        tsc(T.xst[:, 2:640:4], win("xw", 2).indirect(T.mL[:, 0:10]), 2.0, None, [A.mult], xs(2), ["xst2.0"])
        tsc(T.xst[:, 3:1280:4], win("xw", 3).indirect(T.mL[:]), 2.0, None, [A.mult], xs(3), ["xst3"])
        for h in (0, 1): quant(T.tq[:, HF * h:HF * h + HF], T.ts[:, HF * h:HF * h + HF], T.xst[:, 640 * h:640 * h + 640], ["xst0", "xst1", "xst2.%d" % h, "xst3"], ["tq%d" % h])
        if k == 0: quant(T.vq[:], T.vs[:], T.vt[:], ["vt"], ["vq"])

    for h in (0, 1):
        c = slice(HF * h, HF * h + HF)
        mm(6 + h, HF, T.vq[:], T.vs[:], T.tq[:, c], T.ts[:, c], ["vq", "tq%d" % h])
    cp(T.yo[:, 0:HF], bank(6, HF), ["ps6"], ["yo0"])
    act(T.yo[:, HF:C], bank(7, HF), ["ps7"], ["yo1"])
    dma("y", T.oc[:], T.tq[:].bitcast(dt.uint8), ["tq0", "tq1"], [])
    dma("y", T.y[:, 0:HF], T.yo[:, 0:HF], ["yo0"], [])
    dma("s", T.y[:, HF:C], T.yo[:, HF:C], ["yo1"], [])
    for i in range(4): dma("y" if i < 2 else "s", T.osc[4 * i:4 * i + 4, :], T.ts[32 * i:32 * i + 4, :], ["tq0", "tq1"], [])
    for i in range(ndma[0]): need("g", ("x", "dm%d" % i, 16, {}))
    for s, n in cnt.items(): need("g", ("x", s, n, {}))
    for k, n in moved:
        need("g", ("x", "loc%d" % k, n, {}))
        need("g", ("x", "arr%d" % k, n, {}))
